import numpy as np, ml_dtypes
CORES = [51,54,179,182]
N = 4
BF = ml_dtypes.bfloat16
S, M = 3072, 1024
def pack(x, slot, w):
    return {"x": np.clip(np.rint(x), -255, 255).astype(np.int32).astype(np.float32).astype(BF), "slot": slot.astype(np.int32), "w": np.rint(w).astype(np.int32).astype(np.float32)}
def setup_inputs(rng):
    x = rng.standard_normal((N, 128, S), dtype=np.float32) * rng.integers(20, 61, (1, 128, 1)) + rng.integers(-80, 81, (1, 128, 1)) + rng.integers(-15, 16, (N, 128, 1))
    slot = np.floor(M * rng.random((N, 8, S)) ** rng.integers(1, 4, (1, 8, 1))).astype(np.int64) ^ rng.integers(0, M, (1, 8, 1))
    return pack(x, slot, rng.integers(-255, 256, (N, 128, 1)))
def setup_inputs_one(rng):
    d = setup_inputs(rng); e = rng.integers(0, M, (1, 8, 1)); e[0, 0] = 0; e[0, 7] = M - 1
    d["slot"][:] = e; d["w"].reshape(N, 8, 16)[:, ::2] = 0; return d
def setup_inputs_gaps(rng):
    x = np.floor(255 * rng.random((N, 128, S)) ** 4) - 255
    slot = 2 * rng.integers(0, M // 2, (N, 8, S)) + ((np.arange(N)[:, None, None] + np.arange(8)[:, None]) & 1)
    z = rng.integers(0, M, (1, 8, 1)); slot = np.where(slot == z, slot ^ 2, slot)
    slot[0, :, S - 1] = z[0, :, 0]; slot[N - 1, :, 0] = z[0, :, 0]
    x[0, :, S - 1] = rng.integers(-60, 0, 128); x[N - 1, :, 0] = -255
    return pack(x, slot, rng.integers(-255, 256, (N, 128, 1)))
def setup_inputs_ends(rng):
    p = rng.choice(np.array([0, 2.0 ** -6, 2.0 ** -11]), 128); p[0] = 0; p[1] = 2.0 ** -6
    x = np.where(rng.random((N, 128, S)) < p[:, None], 255, -255)
    slot = rng.integers(0, M, (N, 8, S)); slot[:, 1::2] = rng.choice(np.array([0, 1, M - 2, M - 1]), (N, 4, S))
    w = rng.choice(np.array([-255, 255]), (N, 128, 1)); w[:, :16] = 255
    return pack(x, slot, w)
def setup_inputs_spread(rng):
    x = rng.integers(-255, 256, (N, 128, S)) * np.exp2(-rng.integers(0, 9, (N, 1, S)))
    slot = np.floor(M * rng.random((N, 8, S)) ** rng.integers(1, 13, (N, 8, 1))).astype(np.int64) ^ rng.integers(0, M, (1, 8, 1))
    return pack(x, slot, rng.integers(-255, 256, (N, 128, 1)) * np.exp2(-rng.integers(0, 8, (N, 128, 1))))
def check_inputs(d):
    bad = []
    for k in ("x", "w"):
        v = d[k].astype(np.float32)
        if not (np.all(np.abs(v) <= 255) and np.all(v == np.rint(v))): bad.append(k + " whole, -255 to 255")
    if not (np.all(d["slot"] >= 0) and np.all(d["slot"] < M)): bad.append("slot 0 to M - 1")
    return bad
def reference(x, slot, w):
    h = np.arange(8)
    v = np.ascontiguousarray(x.astype(np.float32).astype(np.int64).reshape(N, 8, 16, S).transpose(0, 3, 1, 2)).reshape(N * S, 8, 16)
    s = slot.transpose(0, 2, 1).reshape(N * S, 8)
    c = w.astype(np.int64).reshape(N, 1, 8, 16)
    for layer in range(2):
        if layer == 1: s = np.sum(v.reshape(N, S, 8, 16) * c, axis=3).reshape(N * S, 8) & (M - 1)
        m = np.full((8, M, 16), -256, np.int64); y = np.empty_like(v)
        for t in range(N * S):
            y[t] = np.maximum(m[h, s[t]], v[t]); m[h, s[t]] = y[t]
        v = y
    return {"y": np.ascontiguousarray(v.reshape(N, S, 8, 16).transpose(0, 2, 3, 1)).reshape(N, 128, S).astype(np.float32).astype(BF)}

@@ -1,0 +1,485 @@
+from concourse.bass import DstId, RemoteDMATransfer
+from concourse.mybir import dt, AluOpType, AxisListType, ActivationFunctionType
+
+S_TOK, NC, ND = 3072, 192, 32
+F = NC * ND
+UNIT = 510
+HI = 64 * UNIT
+NEG = -1000000.0
+MAGIC = 12582912.0
+ND_V = (26, 24)
+ND_S = min(ND_V)
+MID = (ND_S + ND) // 2
+EV = 96
+SHIFT = 26440.0
+SP_V = 112
+PC = 1024
+SC_V = 100
+STORE = 2688
+CUT = 1664
+
+SB = {"bfloat16": {"xs": S_TOK, "y1": S_TOK, "yl": S_TOK, "yo": S_TOK, "ones": 288, "ident": 128, "bm": 128, "bt": 128, "lm": 128,
+                   "i192": 128, "cio": NC, "m2": 2048, "m3": 2048, "wm": 2048, "m2l": 2048, "dl": NC, "sq": NC,
+                   "dgm": 128 * (ND - ND_S), "zero": 3072, "dig1": NC, "dig2": NC, "oh": F + 16, "ct": F + 16, "g1": 16 * EV,
+                   "g2": 16 * EV, "mkt": 32, "e1": 1024, "e2": 1024, "e3": 1024, "ext": S_TOK, "tl0": 1024, "tl1": 1024,
+                   "ld00": 1024, "ld01": 1024, "ld02": 1024, "ld10": 1024, "ld11": 1024, "ld12": 1024, "ta": 1024, "tb": 1024},
+      "float32": {"wc": 1, "lane": 1, "ml": 32, "dq": 32, "hi192": 32, "kc": 1024, "jt": 32, "cw": 2, "packed": S_TOK,
+                  "pkb": S_TOK, "krow": S_TOK, "los": S_TOK, "losb": S_TOK, "srt": S_TOK + 8},
+      "int32": {"pi": 1, "li": 1, "ki": NC, "loi": NC, "keyi": NC, "h16": NC, "ji": 32, "jq": 32, "jc": 32},
+      "float16": {"pk": NC, "msk": ND * EV},
+      "uint16": {"koff": NC, "poff": EV, "off1": NC, "off2": NC, "eoff": 64, "lst": 64}}
+SCRATCH = {
+    "sl_i": ("sbuf", [16, 1536], "int32"), "sl_h": ("sbuf", [16, 1536], "float16"), "wd": ("sbuf", [16, 288], "bfloat16"),
+    "e2r": ("sbuf", [1, 1536], "bfloat16"),
+    "psa": ("psum", [128, 1536], "float32"), "psb": ("psum", [128, 1536], "float32"),
+    "acc": ("psum", [128, 512], "float32"), "mis": ("psum", [128, 512], "float32"),
+}
+for _t in SB:
+    for _n in SB[_t]:
+        SCRATCH[_n] = ("sbuf", [128, SB[_t][_n]], _t)
+SEMAPHORES = (["cv", "cs", "cp", "cg", "dx0", "dx1", "ds0", "ds1", "dw", "dz", "da0", "da1", "dy0", "dy1", "dy2", "lo0", "lo1"]
+              + ["r%d%d" % (a, b) for a in range(2) for b in range(3)])
+
+
+def mask_of(engines):
+    return sum(1 << e for e in engines)
+
+
+def rank_program(g, core, T, topo):
+    rank = T.rank_of(core)
+    if rank is None:
+        return
+    A, ACT = AluOpType, ActivationFunctionType
+    V, S, P, Y = g.vector, g.scalar, g.tensor, g.sync
+    queue = {"v": V, "s": S, "p": P, "g": g, "y": Y}
+    count = {"v": 0, "s": 0, "p": 0, "g": 0}
+    seen = {}
+    nranks = len(T.cores)
+    sends = rank < nranks - 1
+
+    def need(q, *toks):
+        best = {}
+        for t in toks:
+            if t is not None:
+                best[t[0]] = max(best.get(t[0], 0), t[1])
+        for s in sorted(best):
+            if seen.get((q, s), 0) < best[s]:
+                queue[q].wait_ge(T.sem[s], best[s])
+                seen[(q, s)] = best[s]
+
+    def done(q, ins):
+        count[q] += 1
+        ins.then_inc(T.sem["c" + q], 1)
+        return ("c" + q, count[q])
+
+    def dma(q, sem, out, in_, *deps):
+        need(q, *deps)
+        queue[q].dma_start(out, in_).then_inc(T.sem[sem], 16)
+        return (sem, 16)
+
+    def ts(out, in0, s1, s2, op0, op1, *deps):
+        need("v", *deps)
+        if op1 is None:
+            return done("v", V.tensor_scalar(out, in0, s1, None, op0))
+        return done("v", V.tensor_scalar(out, in0, s1, s2, op0, op1))
+
+    def tt(out, a, b, op, *deps):
+        need("v", *deps)
+        return done("v", V.tensor_tensor(out, a, b, op))
+
+    def vcopy(out, in_, *deps):
+        need("v", *deps)
+        return done("v", V.tensor_copy(out, in_))
+
+    def fill(ap, c):
+        return done("v", V.memset(ap, c))
+
+    def act(out, in_, *deps):
+        need("s", *deps)
+        return done("s", S.activation(out, in_, ACT.Copy))
+
+    def act2(out, in_, func, bias, scale, *deps):
+        need("s", *deps)
+        return done("s", S.activation(out, in_, func, bias=bias, scale=scale))
+
+    def mm(out, lhsT, rhs, start, stop, *deps):
+        need("p", *deps)
+        return done("p", P.matmul(out, lhsT, rhs, start, stop))
+
+    t_s = [dma("y", "ds0", T.sl_i[0:8, :], T.slot[:, 0:1536]), dma("s", "ds1", T.sl_i[8:16, :], T.slot[:, 1536:3072])]
+    t_x = [dma("y", "dx0", T.xs[:, 0:1536], T.x[:, 0:1536]), dma("s", "dx1", T.xs[:, 1536:3072], T.x[:, 1536:3072])]
+    t_w = dma("y", "dw", T.wc[:], T.w[:])
+
+    f_one = fill(T.ones[:], 1.0)
+    f_m2 = fill(T.m2[:], 0.0)
+    f_m3 = fill(T.m3[:], float(UNIT))
+
+    def sel(out, in_, pattern, op, base, cm, *deps):
+        need("g", *deps)
+        return done("g", g.affine_select(out, in_, pattern, op, 0.0, base, cm))
+
+    c_wd = sel(T.wd[:], T.ones[0:16, :], [[-1, 288]], A.is_equal, 15, 16, f_one)
+    c_id = sel(T.ident[:], T.ones[:, 0:128], [[-1, 128]], A.is_equal, 0, 1)
+    t0 = sel(T.bt[:], T.ones[:, 0:128], [[-16, 8], [0, 16]], A.is_ge, 0, 1)
+    c_b = sel(T.bm[:], T.bt[:], [[16, 8], [0, 16]], A.is_ge, 15, -1, t0)
+    c_lm = sel(T.lm[:], T.bm[:], [[1, 128]], A.is_gt, 0, -1, c_b)
+    c_m3 = sel(T.m3[:], T.m3[:], [[-1, 16], [-16, 8], [0, 16]], A.is_equal, 0, 1, f_m3)
+    c_cio = done("g", g.iota(T.cio[:], [[1, NC]], 0, 0, allow_small_or_imprecise_dtypes=True))
+    done("g", g.iota(T.pi[:], [[0, 1]], 0, 1))
+    done("g", g.iota(T.ml[:], [[0, 2], [1, 16]], 0, 0, allow_small_or_imprecise_dtypes=True))
+    c_io = done("g", g.iota(T.hi192[:], [[NC, 32]], 0, 0, allow_small_or_imprecise_dtypes=True))
+    f_m2l = act(T.m2l[:], T.m2[:], f_m2)
+    c_192 = act2(T.i192[:], T.ident[:], ACT.Silu, 0.0, 192.0, c_id)
+    c_dg = None
+    for i in range(ND - ND_S):
+        c_dg = act2(T.dgm[:, 128 * i:128 * i + 128], T.ident[:], ACT.Copy, 0.0, -2.0 * (ND_S + i - MID), c_id)
+    c_m2 = None
+    for q in range(16):
+        act(T.m2[:, 128 * q + q:128 * q + 128:16], T.bm[:, q:128:16], c_b, f_m2, f_m2l)
+    for q in range(16):
+        c_m2 = act(T.m2l[:, 128 * q + q:128 * q + 128:16], T.lm[:, q:128:16], c_lm, f_m2l)
+
+    t_k = None
+    for i in range(2):
+        v0 = vcopy(T.sl_h[:, 768 * i:768 * i + 768], T.sl_i[:, 768 * i:768 * i + 768], *t_s)
+        for h in range(2):
+            for q in range(16):
+                o, c = 128 * h + 15 - q, 96 * h + 48 * i
+                t_k = mm(T.mis[:, c:c + 48], T.wd[:, o:o + 128], T.sl_h[:, 768 * i + q:768 * i + 768:16], q == 0, q == 15, v0, c_wd)
+    f_zero = fill(T.zero[:], 0.0)
+    fill(T.ct[:, 0:1], -128.0)
+    fill(T.ct[:, F + 1:F + 16], 0.0)
+    fill(T.oh[:, F:F + 16], 0.0)
+    f_end = fill(T.srt[:, 0:8], NEG)
+    for e in range(1, max(MID - ND_S, ND - 1 - MID) + 1):
+        f_end = fill(T.e2r[:, 128 * e:128 * e + 128], float(e * e))
+
+    def low(buf, *deps, c=int(NEG)):
+        need("g", *deps)
+        return done("g", g.iota(buf[:], [[0, S_TOK]], c, 0, allow_small_or_imprecise_dtypes=True))
+
+    need("g", f_zero)
+    g.dma_start(T.losb[:], T.zero[:]).then_inc(T.sem["dz"], 16)
+    z_a = low(T.los, c=0)
+    c_kc = done("g", g.iota(T.kc[:], [[HI, 32], [UNIT, 32]], int(SHIFT), 0, allow_small_or_imprecise_dtypes=True))
+
+    st = {"lane": None, "wm": None, "mx": None, "za": z_a, "zb": ("dz", 16)}
+
+    def off_chip_of(src):
+        r = T.rank_of(src)
+        return [d for d in T.cores[r + 1:] if d not in topo.cores_of(src)]
+
+    def link(src, dst):
+        eng = topo.engines(src, dst)
+        offs = off_chip_of(src)
+        if dst in offs:
+            return eng
+        if offs:
+            eng = [e for e in eng if e not in topo.engines(src, offs[0])]
+        return eng[::2]
+
+    def arrivals(r):
+        return len(link(T.cores[r], core))
+
+    def nothing(*a):
+        return None
+
+    def sort_pass(nd, dig, off, dep, ps_free, early_v, inter, hook2, hook1, fillers, late):
+        mm(T.acc[:, 256:256 + EV], T.i192[:], dig[:, 1:NC:2], True, False, dep, c_192)
+        t_po = mm(T.acc[:, 256:256 + EV], T.ident[:], T.cio[:, 1:NC:2], False, True, c_id, c_cio)
+        t_dl = act2(T.dl[:], dig, ACT.Copy, -float(MID), 1.0, dep)
+        t_sq = act2(T.sq[:], dig, ACT.Square, -float(MID), 1.0, dep)
+        v_oh, v_po = None, None
+        for d in range(nd):
+            if d == 4:
+                early_v()
+            if d == 12:
+                v_po = vcopy(T.poff[:], T.acc[:, 256:256 + EV], t_po)
+            v_oh = ts(T.oh[:, NC * d:NC * d + NC], dig, float(d), None, A.is_equal, None, dep)
+        f_v, f_s = NC * nd, F - NC * nd
+        n = f_s // 512 + (f_s % 512 > 0)
+        relu, s_oh = list(ps_free), None
+        for b in range(n):
+            o, w, c, t = 512 * (b % 3), min(512, f_s - 512 * b), 512 * b, None
+            while c < 512 * b + w:
+                i = c // NC
+                m = min(NC * (i + 1), 512 * b + w)
+                e, j = nd + i - MID, nd + i - ND_S
+                z, k = T.psa[:, o + c - 512 * b:o + m - 512 * b], c - NC * i
+                if e:
+                    mm(z, T.dgm[:, 128 * j:128 * j + 128], T.dl[:, k:k + m - c], True, False, t_dl, c_dg, relu[b % 3])
+                    mm(z, T.e2r[:, 128 * abs(e):128 * abs(e) + 128], T.ones[0:1, 0:m - c], False, False, f_end)
+                t = mm(z, T.ident[:], T.sq[:, k:k + m - c], e == 0, True, t_sq, c_id, relu[b % 3])
+                c = m
+            if b == n - 1:
+                inter()
+            s_oh = act2(T.oh[:, f_v + 512 * b:f_v + 512 * b + w], T.psa[:, o:o + w], ACT.Relu, 1.0, -1.0, t, f_end)
+            relu[b % 3] = s_oh
+        sc, c, tok = None, 0, {}
+        while c < F:
+            w = min(3072, (f_v if c < f_v else F) - c)
+            need("v", v_oh, sc, s_oh if c >= f_v else None)
+            init = -128.0 if c == 0 else T.ct[:, c:c + 1]
+            sc = done("v", V.tensor_tensor_scan(T.ct[:, c + 1:c + w + 1], T.oh[:, c:c + w], T.zero[:, 0:w], init, A.add, A.add))
+            c += w
+            tok[c] = sc
+        bank = list(relu)
+
+        def early(b):
+            z, a = T.psa[:, 512 * (b % 3):512 * (b % 3) + 512], 1024 * b
+            mm(z, T.lm[:], T.oh[:, a:a + 1024:2], True, False, v_oh, s_oh if a + 1024 > f_v else None, c_lm, bank[b % 3])
+
+        for b in range(3):
+            early(b)
+        hook2()
+        need("s", v_oh, s_oh, v_po)
+        s_2 = done("s", S.activation(T.g2[:], T.oh[:].indirect(T.poff[:]), ACT.Copy))
+        need("s", sc)
+        s_1 = done("s", S.activation(T.g1[:], T.ct[:].indirect(T.poff[:]), ACT.Copy))
+        hook1()
+        red, d, t = [], 0, None
+        for b in range(6):
+            z, a = T.psa[:, 512 * (b % 3):512 * (b % 3) + 512], 1024 * b
+            if b > 2:
+                early(b)
+            t = tok[min(k for k in tok if k >= a + 1024)]
+            t = mm(z, T.bm[:], T.ct[:, a:a + 1024:2], False, True, t, c_b)
+            bank[b % 3] = tt(T.msk[:, 512 * b:512 * b + 512], z, T.oh[:, a:a + 1024:2], A.mult, t)
+            red.append(bank[b % 3])
+            if b == 2:
+                fillers(sc)
+                for q in range(16):
+                    mm(T.mis[:, 256:256 + EV], T.m2l[:, 128 * q:128 * q + 128], T.g2[:, q:16 * EV:16], q == 0, False, s_2, c_m2)
+            if b in (2, 4, 5):
+                while EV * (d + 1) <= 512 * (b - 1):
+                    mm(T.acc[:, 0:EV], T.ident[:], T.msk[:, EV * d:EV * d + EV], d == 0, False, red[b - 2])
+                    d += 1
+        t_o = None
+        for q in range(16):
+            t_o = mm(T.mis[:, 256:256 + EV], T.m2[:, 128 * q:128 * q + 128], T.g1[:, q:16 * EV:16], False, q == 15, s_1)
+        while d < ND:
+            t = mm(T.acc[:, 0:EV], T.ident[:], T.msk[:, EV * d:EV * d + EV], False, d == ND - 1, red[min(5, (EV * d + EV - 1) // 512)])
+            d += 1
+        late()
+        ts(off[:, 1:NC:2], T.mis[:, 256:256 + EV], 2048.0, None, A.add, None, t_o)
+        return ts(off[:, 0:NC:2], T.acc[:, 0:EV], 2048.0, None, A.add, None, t), sc, bank
+
+    def layer(li, src, src_toks, key_tok, out, piece_done):
+        v = vcopy(T.ki[:], T.mis[:, 0:NC], key_tok)
+        v_lo = ts(T.loi[:], T.ki[:], 31, None, A.bitwise_and, None, v)
+        v_d1 = vcopy(T.dig1[:], T.loi[:], v_lo)
+        kt, t_p, jt, pb, ko = {}, [], [None], [], []
+
+        def pack_keys():
+            a = ts(T.keyi[:], T.ki[:], 1023, None, A.bitwise_and, None, v)
+            b = ts(T.h16[:], T.ki[:], 992, None, A.bitwise_and, None, v)
+            kt["pk"] = tt(T.pk[:], T.keyi[:], T.h16[:], A.add, a, b)
+            kt["key"] = a
+
+        def row_bank(ps, b, c, with_src, *deps):
+            t = None
+            if with_src:
+                mm(ps[:, 512 * b:512 * b + 512], T.ident[:], src[:, c:c + 512], True, False, c_id, *(deps + tuple(src_toks)))
+            for q in range(16):
+                t = mm(ps[:, 512 * b + q:512 * b + 512:16], T.m3[:, 128 * q:128 * q + 128], T.pk[:, c // 16:c // 16 + 32],
+                       not with_src, q == 15 or not with_src, kt["pk"], c_m3, *deps)
+            return t
+
+        def pack_p(i, free):
+            pb.append(row_bank(T.psb, i % 3, 512 * i, True, free))
+
+        def pack_s(i):
+            t_p.append(act2(T.packed[:, 512 * i:512 * i + 512], T.psb[:, 512 * (i % 3):512 * (i % 3) + 512], ACT.Copy, SHIFT, 1.0,
+                            pb[i], st["mx"]))
+
+        def packs_x():
+            for i in range(3):
+                pack_p(i, None)
+
+        def packs_y():
+            for i in range(3):
+                pack_s(i)
+            pack_p(3, t_p[0])
+
+        def packs_z():
+            pack_s(3)
+
+        def packs_l():
+            for i in (4, 5):
+                pack_p(i, t_p[i - 3])
+                pack_s(i)
+
+        def fillers(sc):
+            if sends:
+                jt[0] = mm(T.mis[:, 0:32], T.bm[:], T.ct[:, NC:F + 1:NC], True, True, sc)
+            ko.append(vcopy(T.koff[:], T.keyi[:], kt["key"]))
+            if st["lane"] is None:
+                a = ts(T.li[:], T.pi[:], 15, None, A.bitwise_and, None, c_io)
+                a = vcopy(T.lane[:], T.li[:], a)
+                st["lane"] = ts(T.dq[:], T.ml[:], T.lane[:], None, A.is_equal, None, a)
+
+        g_b = low(T.pkb, st["mx"])
+        v_o1, _, psa_t = sort_pass(ND_V[0], T.dig1[:], T.off1, v_d1, [None] * 3, pack_keys, packs_x, packs_y, packs_z, fillers,
+                                   packs_l)
+        need("v", v_o1, st["za"], *t_p[:(16 * SP_V + 511) // 512])
+        v_s1 = done("v", V.tensor_copy(T.los[:].indirect(T.off1[:, 0:SP_V]), T.packed[:, 0:16 * SP_V]))
+        need("s", v_o1, st["zb"], *t_p)
+        s_s1 = done("s", S.activation(T.losb[:].indirect(T.off1[:, SP_V:NC]), T.packed[:, 16 * SP_V:], ACT.Silu))
+        pk_r = [None, None]
+
+        def key_mm(h, *deps):
+            for b in range(3):
+                pk_r[h] = row_bank((T.psa, T.psb)[h], b, 1536 * h + 512 * b, False, *deps)
+
+        def key_rows(h):
+            return act2(T.krow[:, 1536 * h:1536 * h + 1536], (T.psa, T.psb)[h][:], ACT.Copy, SHIFT, 1.0, pk_r[h])
+
+        key_mm(1, *t_p[3:6])
+        t_hi, v_j, sc_hi = None, None, 1.0 / (16.0 * HI)
+        if sends:
+            v_j = ts(T.ji[:], T.mis[:, 0:32], 2048.0, None, A.add, None, jt[0], v_o1)
+        need("v", v_s1)
+        need("s", s_s1)
+        t_da = ("da%d" % li, 16)
+        for c in range(S_TOK - PC, -1, -PC):
+            e_a = ts(T.ext[:, c:c + PC], T.los[:, c:c + PC], sc_hi, None, A.mult, None)
+            e_b = act2(T.yo[:, c:c + PC], T.losb[:, c:c + PC], ACT.Copy, 0.0, sc_hi)
+            if c <= 16 * SC_V < c + PC:
+                need("g", e_a, s_s1)
+                g.dma_start(T.los[:, 16 * SC_V:], T.losb[:, 16 * SC_V:], accum_op=A.add).then_inc(T.sem[t_da[0]], 16)
+            for last, x, t in ((False, T.ext, e_a), (True, T.yo, e_b)):
+                for q in range(16):
+                    t_hi = mm(T.mis[:, c // 16:(c + PC) // 16], T.m2[:, 128 * q:128 * q + 128], x[:, c + q:c + PC:16],
+                              q == 0 and not last, q == 15 and last, t, c_m2, v_j)
+        g_a = low(T.packed, v_s1, s_s1)
+        t_kr = [None, None]
+        t_mk = None
+        if sends:
+            v_q = ts(T.jq[:], T.ji[:], 15, None, A.bitwise_and, None, v_j)
+            v_c = ts(T.jc[:], T.ji[:], 4, None, A.logical_shift_right, None, v_j)
+            t_mk = ts(T.mkt[:], T.jq[:], T.lane[:], None, A.is_gt, None, v_q, st["lane"])
+            v = tt(T.jt[:], T.jc[:], T.dq[:], A.mult, v_c, st["lane"])
+            need("v", v)
+            for b in range(2):
+                v = done("v", V.tensor_reduce(T.cw[:, b:b + 1], T.jt[:, 16 * b:16 * b + 16], AxisListType.X, A.add))
+        v_d2 = ts(T.dig2[:], T.mis[:, 0:NC], MAGIC, MAGIC + 1.0, A.add, A.subtract, t_hi)
+
+        def lists(sc):
+            if sends:
+                for b in range(2):
+                    kt["l"] = ts(T.lst[:, b:64:2], T.hi192[:], T.cw[:, b:b + 1], None, A.add, None, v, c_io)
+
+        v_o2, v_ct, _ = sort_pass(ND_V[1], T.dig2[:], T.off2, v_d2, [None] * 3, nothing, nothing, nothing, nothing, lists, nothing)
+        t_e, p, ps_a = None, None, v_o2
+        if sends:
+            need("s", kt["l"], v_ct)
+            s_1 = done("s", S.activation(T.e1[:], T.ct[:].indirect(T.lst[:]), ACT.Copy))
+            s_2 = done("s", S.activation(T.e2[:], T.oh[:].indirect(T.lst[:]), ACT.Copy))
+            for q in range(16):
+                mm(T.mis[:, 0:64], T.m2[:, 128 * q:128 * q + 128], T.e1[:, q:1024:16], q == 0, False, s_1, v_o2)
+            for b in range(2):
+                mm(T.psa[:, 512 * b:512 * b + 512], T.ident[:], T.e2[:, 512 * b:512 * b + 512], True, False, s_2, v_o2)
+                for i in range(16):
+                    c = 512 * b + 32 * i
+                    p = mm(T.psa[:, c:c + 32], T.ident[:], T.mkt[:], False, i == 15, t_mk)
+        need("v", v_o2, g_a, v_s1, s_s1)
+        v = done("v", V.tensor_tensor(T.packed[:].indirect(T.off2[:, 0:SC_V]), T.los[:, 0:16 * SC_V], T.losb[:, 0:16 * SC_V], A.add))
+        need("s", v_o2, g_b, t_da)
+        s_w = done("s", S.activation(T.pkb[:].indirect(T.off2[:, SC_V:NC]), T.los[:, 16 * SC_V:], ACT.Silu))
+        if sends:
+            s_3 = ps_a = act2(T.e3[:], T.psa[:, 0:1024], ACT.Relu, -1.0, 1.0, p)
+            for q in range(16):
+                t_e = mm(T.mis[:, 0:64], T.m2[:, 128 * q:128 * q + 128], T.e3[:, q:1024:16], False, q == 15, s_3)
+        key_mm(0, ps_a)
+        t_kr[1] = key_rows(1)
+        need("v", v, s_w)
+        v_mx = done("v", V.tensor_tensor_scan(T.srt[:, 8:], T.packed[:], T.pkb[:], NEG, A.max, A.max))
+        st["mx"] = v_mx
+        tl = T["tl%d" % li]
+        if sends:
+            v_e = ts(T.eoff[:], T.mis[:, 0:64], 2055.0, None, A.add, None, t_e)
+            v_t = tt(tl[:], T.srt[:].indirect(T.eoff[:]), T.kc[:], A.subtract, v_mx, v_e, c_kc)
+            need("g", v_t)
+            off_chip = off_chip_of(core)
+            on_chip = [d for d in T.cores[rank + 1:] if d not in off_chip]
+            total = 0
+            for group in [c for c in (off_chip[:1], on_chip + off_chip[1:]) if c]:
+                trans = []
+                for d in group:
+                    eng = link(core, d)
+                    total += len(eng)
+                    rid, pid = topo.addr(d, core)
+                    trans.append(RemoteDMATransfer(dst_ids=[DstId(rid=rid, pnc=pid)], dma_engine_mask=mask_of(eng),
+                                                   remote_sem=T.sem["r%d%d" % (li, rank)], srcs=[tl[:]],
+                                                   dsts=[T["ld%d%d" % (li, rank)][:]]))
+                g.remote_dma_fused(trans, local_sem=T.sem["lo%d" % li])
+            st["lo%d" % li] = total
+        if li == 0:
+            st["zb"] = low(T.losb, v_mx, c=0)
+        a = 64 if sends else 96
+        need("v", v_mx)
+        v_a = done("v", V.tensor_copy(T.los[:, 0:16 * a], T.srt[:, 8:].indirect(T.off2[:, 0:a])))
+        need("s", v_mx)
+        s_a = done("s", S.activation(T.los[:, 16 * a:], T.srt[:, 8:].indirect(T.off2[:, a:NC]), ACT.Copy))
+        t_kr[0] = key_rows(0)
+        if st["wm"] is None:
+            st["wm"] = act2(T.wm[:], T.m2[:], ACT.Copy, 0.0, T.wc[:], c_m2, t_w)
+        dst = T.yl if rank > 0 else out
+        ys = []
+        for c, e in ((CUT, S_TOK), (0, CUT)):
+            need("v", v_a, s_a, t_kr[1], t_kr[0] if c < 1536 else None)
+            ys.append(done("v", V.tensor_tensor(dst[:, c:e], T.los[:].indirect(T.off1[:, c // 16:e // 16]), T.krow[:, c:e], A.subtract)))
+            if rank == 0:
+                for i, j in ((CUT, STORE), (STORE, S_TOK)) if c else ((0, CUT),):
+                    piece_done(i, j, ys[-1])
+        if li == 0:
+            st["za"] = low(T.los, *ys, c=0)
+        if rank > 0:
+            parts, c = [], CUT
+            for ps, o in ((T.acc, 0), (T.psa, 1024), (T.psb, 1024)):
+                n = min(512, S_TOK - c)
+                t = mm(ps[:, o:o + n], T.ident[:], T.yl[:, c:c + n], True, True, ys[0], t_kr[0], t_kr[1])
+                parts.append((ps, o, c, n, t))
+                c += n
+            tin = T["ld%d0" % li]
+            v_in = ("r%d0" % li, arrivals(0))
+            merge = []
+            for r in range(1, rank):
+                ps = (T.psa, T.psb)[r % 2]
+                for b in range(2):
+                    t = mm(ps[:, 512 * b:512 * b + 512], T.ident[:], T["ld%d%d" % (li, r)][:, 512 * b:512 * b + 512], True, True,
+                           ("r%d%d" % (li, r), arrivals(r)), ps_a, t_kr[0])
+                merge.append(((T.ta, T.tb)[r % 2], ps, t))
+            for nxt, ps, t in merge:
+                v_in = tt(nxt[:], ps[:, 0:1024], tin[:], A.max, t, v_in)
+                tin = nxt
+            need("s", v_in, ko[0])
+            s_t = done("s", S.activation(T.ext[:, CUT:], tin[:].indirect(T.koff[:, CUT // 16:]), ACT.Copy))
+            piece_done(0, CUT, tt(out[:, 0:CUT], tin[:].indirect(T.koff[:, 0:CUT // 16]), T.yl[:, 0:CUT], A.max, v_in, ys[1], ko[0]))
+            for ps, o, c, n, t in parts:
+                v = tt(out[:, c:c + n], ps[:, o:o + n], T.ext[:, c:c + n], A.max, t, s_t)
+                if c + n == STORE:
+                    piece_done(CUT, STORE, v)
+            piece_done(STORE, S_TOK, v)
+
+    hk = []
+
+    def hash_piece(c, e, tok):
+        t = None
+        for q in range(16):
+            t = mm(T.mis[:, c // 16:e // 16], T.wm[:, 128 * q:128 * q + 128], T.y1[:, c + q:e:16], q == 0, q == 15, tok, st["wm"])
+        hk.append((tok, t))
+
+    def store_piece(c, e, tok):
+        dma("y", {0: "dy0", CUT: "dy1"}.get(c, "dy2"), T.y[:, c:e], T.yo[:, c:e], tok)
+
+    layer(0, T.xs, t_x, t_k, T.y1, hash_piece)
+    layer(1, T.y1, [h[0] for h in hk], max(h[1] for h in hk), T.yo, store_piece)
+
+    for q in ("v", "s", "p", "g"):
+        need("g", ("c" + q, count[q]))
+    for s in ("ds0", "ds1", "dx0", "dx1", "dw", "dz", "da0", "da1", "dy0", "dy1", "dy2"):
+        need("g", (s, 16))
+    if sends:
+        for li in range(2):
+            need("g", ("lo%d" % li, st["lo%d" % li]))

@@ -1,43 +1,58 @@
 from concourse.bass import DstId, RemoteDMATransfer
 from concourse.mybir import dt, AluOpType, AxisListType, ActivationFunctionType
 
-S_TOK, NC, ND = 3072, 192, 32
-F = NC * ND
+S_TOK, NC, ND, BL = 3072, 192, 32, 12
+NT = ND * BL
 UNIT = 510
 HI = 64 * UNIT
 NEG = -1000000.0
-MAGIC = 12582912.0
-ND_V = (26, 24)
-ND_S = min(ND_V)
-MID = (ND_S + ND) // 2
-EV = 96
-SHIFT = 26440.0
-SP_V = 112
+MAGIC = 393216.0
+SHIFT = 26440
+LIFT = 34
+MIDP = 1536.0
+SP_V = 96
 PC = 1024
-SC_V = 100
-STORE = 2688
-CUT = 1664
+SC_V = 98
+CUT = 16 * SP_V
+STORE = CUT + 1024
+BLOCKS = {"first": (9, 5, 12), "lo": (9, 5, 12), "hi": (9, 5, 12), "ends": (7, 5, 11)}
+LV = 9
+ZB = 1024
+FOLD, STEP = False, (2, 2)
+W = 2
+GROUPS = (10, 8, 8, 6)
+PAIR_S = {"first": 0, "lo": 1, "hi": 2}
+DF, ID, I384, RD, LM, GE, BM, M3, NM = 0, 8, 9, 10, 18, 19, 20, 21, 37
+PACK = (("table", "table", "table"), ("group3", "starts", "table"))
+COPY = ({"tail": (0, 3)}, {"starts": (0, 1), "tail": (1, 3)})
 
-SB = {"bfloat16": {"xs": S_TOK, "y1": S_TOK, "yl": S_TOK, "yo": S_TOK, "ones": 288, "ident": 128, "bm": 128, "bt": 128, "lm": 128,
-                   "i192": 128, "cio": NC, "m2": 2048, "m3": 2048, "wm": 2048, "m2l": 2048, "dl": NC, "sq": NC,
-                   "dgm": 128 * (ND - ND_S), "zero": 3072, "dig1": NC, "dig2": NC, "oh": F + 16, "ct": F + 16, "g1": 16 * EV,
-                   "g2": 16 * EV, "mkt": 32, "e1": 1024, "e2": 1024, "e3": 1024, "ext": S_TOK, "tl0": 1024, "tl1": 1024,
+SB = {"bfloat16": {"xs": S_TOK, "y1": S_TOK, "yl": CUT, "yo": S_TOK, "ext": S_TOK, "ones": NC,
+                   "zero": NT, "dig1": W * NC, "dig2": W * NC, "cmod": NC, "eq": 1536, "run": NT + 16, "lsel": 16, "mkb": NC * LV,
+                   "mk": 32, "mkl": 32, "cc": 64, "dsel": 32, "mrep": 1024, "e3": 1024, "tl0": 1024, "tl1": 1024,
                    "ld00": 1024, "ld01": 1024, "ld02": 1024, "ld10": 1024, "ld11": 1024, "ld12": 1024, "ta": 1024, "tb": 1024},
-      "float32": {"wc": 1, "lane": 1, "ml": 32, "dq": 32, "hi192": 32, "kc": 1024, "jt": 32, "cw": 2, "packed": S_TOK,
-                  "pkb": S_TOK, "krow": S_TOK, "los": S_TOK, "losb": S_TOK, "srt": S_TOK + 8},
-      "int32": {"pi": 1, "li": 1, "ki": NC, "loi": NC, "keyi": NC, "h16": NC, "ji": 32, "jq": 32, "jc": 32},
-      "float16": {"pk": NC, "msk": ND * EV},
-      "uint16": {"koff": NC, "poff": EV, "off1": NC, "off2": NC, "eoff": 64, "lst": 64}}
+      "float32": {"wc": 1, "wc32": 1, "lane": 2, "one8": 8, "hm0": 8, "hm": 8, "lmk": 16, "hi192": 32, "kc0": 1024, "kc1": 1024,
+                  "jt": 32, "ju": 32, "ys": NT, "tab": NT, "packed": S_TOK - CUT, "pka": S_TOK, "pkb": S_TOK, "krow": CUT,
+                  "x32": CUT, "pg": S_TOK - CUT, "i32": 256, "los": S_TOK, "losb": S_TOK, "srt": S_TOK + 8},
+      "int32": {"sl_i": NC, "pi": 1, "li": 1, "ri": NC, "hii": NC, "ji": 32, "cb": 32, "lb": 32},
+      "float16": {"kf": NC, "pk": NC - SP_V, "gb": S_TOK, "e1": 1024},
+      "uint16": {"koff": NC, "poff": NC, "off1": NC, "off2": NC, "eoff": 64, "lst": 64, "ls2": 2}}
 SCRATCH = {
-    "sl_i": ("sbuf", [16, 1536], "int32"), "sl_h": ("sbuf", [16, 1536], "float16"), "wd": ("sbuf", [16, 288], "bfloat16"),
-    "e2r": ("sbuf", [1, 1536], "bfloat16"),
+    "zm": ("sbuf", [128, 144], "bfloat16"), "zw": ("sbuf", [128, 144], "bfloat16"), "sl_h": ("sbuf", [128, BL, 16], "float16"),
+    "sl_x": ("sbuf", [128, BL, 128], "float16"), "oh": ("sbuf", [128, ND, NC], "bfloat16"),
+    "sm": ("sbuf", [128, NM, 16], "bfloat16"), "cm": ("sbuf", [128, NM, 128], "bfloat16"),
+    "mrow": ("sbuf", [128, 8, 16], "bfloat16"), "row1": ("sbuf", [128, 8, 16], "bfloat16"),
+    "urow": ("sbuf", [128, 8, 16], "bfloat16"), "vrow": ("sbuf", [128, 8, 16], "int32"),
+    "tma": ("sbuf", [128, 8, 16], "bfloat16"), "tmb": ("sbuf", [128, 8, 16], "bfloat16"),
+    "tmc": ("sbuf", [128, 8, 16], "bfloat16"),
+    "hrow": ("sbuf", [1, 1024], "bfloat16"), "n32": ("sbuf", [1, 128], "bfloat16"),
     "psa": ("psum", [128, 1536], "float32"), "psb": ("psum", [128, 1536], "float32"),
     "acc": ("psum", [128, 512], "float32"), "mis": ("psum", [128, 512], "float32"),
 }
 for _t in SB:
     for _n in SB[_t]:
         SCRATCH[_n] = ("sbuf", [128, SB[_t][_n]], _t)
-SEMAPHORES = (["cv", "cs", "cp", "cg", "dx0", "dx1", "ds0", "ds1", "dw", "dz", "da0", "da1", "dy0", "dy1", "dy2", "lo0", "lo1"]
+LOCAL = ["dx0", "dx1", "ds", "dw", "da00", "da01", "da10", "da11"]
+SEMAPHORES = (["cv", "cs", "cp", "cg", "lo0", "lo1", "dy0", "dy1", "dy2", "dy3"] + LOCAL
               + ["r%d%d" % (a, b) for a in range(2) for b in range(3)])
 
 
@@ -91,395 +106,443 @@ def rank_program(g, core, T, topo):
         need("v", *deps)
         return done("v", V.tensor_copy(out, in_))
 
+    def scan(out, a, b, init, op0, op1, *deps):
+        need("v", *deps)
+        return done("v", V.tensor_tensor_scan(out, a, b, init, op0, op1))
+
     def fill(ap, c):
         return done("v", V.memset(ap, c))
 
-    def act(out, in_, *deps):
-        need("s", *deps)
-        return done("s", S.activation(out, in_, ACT.Copy))
-
-    def act2(out, in_, func, bias, scale, *deps):
+    def act(out, in_, func, bias, scale, *deps):
         need("s", *deps)
         return done("s", S.activation(out, in_, func, bias=bias, scale=scale))
+
+    def sgat(out, in_, func, *deps):
+        need("s", *deps)
+        return done("s", S.activation(out, in_, func))
 
     def mm(out, lhsT, rhs, start, stop, *deps):
         need("p", *deps)
         return done("p", P.matmul(out, lhsT, rhs, start, stop))
 
-    t_s = [dma("y", "ds0", T.sl_i[0:8, :], T.slot[:, 0:1536]), dma("s", "ds1", T.sl_i[8:16, :], T.slot[:, 1536:3072])]
-    t_x = [dma("y", "dx0", T.xs[:, 0:1536], T.x[:, 0:1536]), dma("s", "dx1", T.xs[:, 1536:3072], T.x[:, 1536:3072])]
+    def sel(out, in_, pattern, op, other, base, cm, *deps):
+        need("g", *deps)
+        return done("g", g.affine_select(out, in_, pattern, op, other, base, cm))
+
+    def low(out, pattern, base, cm=0, *deps):
+        need("g", *deps)
+        return done("g", g.iota(out, pattern, base, cm, allow_small_or_imprecise_dtypes=True))
+
+    def C(j):
+        return T.cm[:, j, :]
+
+    def to_lane(z, q):
+        return z[:, 15 - q:143 - q]
+
+    t_s = dma("y", "ds", T.sl_i[:], T.slot[:])
+    t_x0 = dma("y", "dx0", T.xs[:, 0:CUT], T.x[:, 0:CUT])
+    t_x = dma("y", "dx1", T.xs[:, CUT:], T.x[:, CUT:])
     t_w = dma("y", "dw", T.wc[:], T.w[:])
 
-    f_one = fill(T.ones[:], 1.0)
-    f_m2 = fill(T.m2[:], 0.0)
-    f_m3 = fill(T.m3[:], float(UNIT))
-
-    def sel(out, in_, pattern, op, base, cm, *deps):
-        need("g", *deps)
-        return done("g", g.affine_select(out, in_, pattern, op, 0.0, base, cm))
-
-    c_wd = sel(T.wd[:], T.ones[0:16, :], [[-1, 288]], A.is_equal, 15, 16, f_one)
-    c_id = sel(T.ident[:], T.ones[:, 0:128], [[-1, 128]], A.is_equal, 0, 1)
-    t0 = sel(T.bt[:], T.ones[:, 0:128], [[-16, 8], [0, 16]], A.is_ge, 0, 1)
-    c_b = sel(T.bm[:], T.bt[:], [[16, 8], [0, 16]], A.is_ge, 15, -1, t0)
-    c_lm = sel(T.lm[:], T.bm[:], [[1, 128]], A.is_gt, 0, -1, c_b)
-    c_m3 = sel(T.m3[:], T.m3[:], [[-1, 16], [-16, 8], [0, 16]], A.is_equal, 0, 1, f_m3)
-    c_cio = done("g", g.iota(T.cio[:], [[1, NC]], 0, 0, allow_small_or_imprecise_dtypes=True))
-    done("g", g.iota(T.pi[:], [[0, 1]], 0, 1))
-    done("g", g.iota(T.ml[:], [[0, 2], [1, 16]], 0, 0, allow_small_or_imprecise_dtypes=True))
-    c_io = done("g", g.iota(T.hi192[:], [[NC, 32]], 0, 0, allow_small_or_imprecise_dtypes=True))
-    f_m2l = act(T.m2l[:], T.m2[:], f_m2)
-    c_192 = act2(T.i192[:], T.ident[:], ACT.Silu, 0.0, 192.0, c_id)
-    c_dg = None
-    for i in range(ND - ND_S):
-        c_dg = act2(T.dgm[:, 128 * i:128 * i + 128], T.ident[:], ACT.Copy, 0.0, -2.0 * (ND_S + i - MID), c_id)
-    c_m2 = None
-    for q in range(16):
-        act(T.m2[:, 128 * q + q:128 * q + 128:16], T.bm[:, q:128:16], c_b, f_m2, f_m2l)
-    for q in range(16):
-        c_m2 = act(T.m2l[:, 128 * q + q:128 * q + 128:16], T.lm[:, q:128:16], c_lm, f_m2l)
-
-    t_k = None
-    for i in range(2):
-        v0 = vcopy(T.sl_h[:, 768 * i:768 * i + 768], T.sl_i[:, 768 * i:768 * i + 768], *t_s)
-        for h in range(2):
-            for q in range(16):
-                o, c = 128 * h + 15 - q, 96 * h + 48 * i
-                t_k = mm(T.mis[:, c:c + 48], T.wd[:, o:o + 128], T.sl_h[:, 768 * i + q:768 * i + 768:16], q == 0, q == 15, v0, c_wd)
+    f_8 = fill(T.one8[:], 1.0)
+    fill(T.zm[:], 0.0)
+    fill(T.zw[:], 0.0)
+    fill(T.sm[:, BM, :], 1.0)
     f_zero = fill(T.zero[:], 0.0)
-    fill(T.ct[:, 0:1], -128.0)
-    fill(T.ct[:, F + 1:F + 16], 0.0)
-    fill(T.oh[:, F:F + 16], 0.0)
-    f_end = fill(T.srt[:, 0:8], NEG)
-    for e in range(1, max(MID - ND_S, ND - 1 - MID) + 1):
-        f_end = fill(T.e2r[:, 128 * e:128 * e + 128], float(e * e))
+    g_pi = low(T.pi[:], [[0, 1]], 0, 1)
+    g_m = low(T.mrow[:], [[0, 8], [1, 16]], 0)
+    t = sel(T.hm0[:], T.one8[:], [[-16, 8]], A.is_ge, 0.0, 0, 1, f_8)
+    g_v = low(T.vrow[:], [[1, 8], [1, 16]], 1)
+    g_u = low(T.urow[:], [[-1, 8], [1, 16]], -1)
+    c_hm = sel(T.hm[:], T.hm0[:], [[16, 8]], A.is_ge, 0.0, 15, -1, t)
+    g_r = sel(T.row1[:], T.mrow[:], [[-1, 8], [-1, 16]], A.is_ge, -1.0, 14, 0, g_m)
+    g_q = low(T.sm[:, M3:NM, :], [[1, 16], [0, 16]], 0)
+    st = {"wm": None, "mkb": None, "mx": None}
+    c_kc = [low(T.kc0[:], [[HI, 32], [UNIT, 32]], SHIFT)]
+    c_cm = low(T.cmod[:], [[0, 16], [1, BL]], 0)
+    st["za"] = low(T.los[:], [[0, S_TOK]], 0)
+    st["zb"] = low(T.losb[:], [[0, S_TOK]], 0)
+    low(T.hi192[:], [[NC, 32]], 0)
+    c_hi = low(T.hrow[:], [[1, 32], [0, 32]], 0)
+    low(T.pka[:, 0:ZB], [[0, ZB]], 0)
 
-    def low(buf, *deps, c=int(NEG)):
-        need("g", *deps)
-        return done("g", g.iota(buf[:], [[0, S_TOK]], c, 0, allow_small_or_imprecise_dtypes=True))
+    def spread(j0, j1, *deps):
+        t = None
+        for h in range(8):
+            t = act(T.cm[:, j0:j1, 16 * h:16 * h + 16], T.sm[:, j0:j1, :], ACT.Copy, 0.0, T.hm[:, h:h + 1], c_hm, *deps)
+        return t
 
-    need("g", f_zero)
-    g.dma_start(T.losb[:], T.zero[:]).then_inc(T.sem["dz"], 16)
-    z_a = low(T.los, c=0)
-    c_kc = done("g", g.iota(T.kc[:], [[HI, 32], [UNIT, 32]], int(SHIFT), 0, allow_small_or_imprecise_dtypes=True))
+    t = ts(T.li[:], T.pi[:], 15, None, A.bitwise_and, None, g_pi)
+    v_l = vcopy(T.lane[:, 0:1], T.li[:], t)
+    v_l2 = ts(T.lane[:, 1:2], T.li[:], -16.0, None, A.add, None, t)
+    lane = T.lane[:, 0:1]
+    v_v = ts(T.vrow[:], T.vrow[:], 15, None, A.bitwise_and, None, g_v)
+    v_a = ts(T.tma[:], T.mrow[:], lane, None, A.is_equal, None, v_l, g_m)
+    s_i = act(T.sm[:, I384, :], T.tma[:, 0, :], ACT.Silu, 0.0, float(NT), v_a)
+    c_ls = ts(T.lsel[:], T.mrow[:, 0, :], lane, 1.0 / 32, A.is_equal, A.mult)
+    ts(T.sm[:, ID, :], T.mrow[:, 0, :], lane, None, A.is_equal, None)
+    ts(T.sm[:, LM, :], T.mrow[:, 0, :], lane, None, A.is_gt, None)
+    ts(T.sm[:, GE, :], T.mrow[:, 0, :], lane, None, A.is_le, None)
+    c_lk = ts(T.lmk[:], T.mrow[:, 0, :], lane, None, A.is_equal, None)
+    v_b = ts(T.tmb[:], T.vrow[:], lane, None, A.is_equal, None, v_v)
+    v0 = vcopy(T.sl_h[:], T.sl_i[:], t_s)
+    u = ts(T.tmc[:], T.urow[:], T.lane[:, 1:2], -1.0, A.is_equal, A.mult, g_u, v_l2)
+    w = ts(T.sm[:, RD:RD + 8, :], T.row1[:], lane, -1.0, A.is_equal, A.mult, g_r)
+    tt(T.sm[:, DF:DF + 8, :], T.tma[:], T.tmb[:], A.subtract, v_b)
+    for h in range(8):
+        t = ts(T.sl_x[:, :, 16 * h:16 * h + 16], T.sl_h[:], T.hm[:, h:h + 1], None, A.mult, None, v0, c_hm)
+        if h == 2:
+            tt(T.sm[:, RD:RD + 7, :], T.sm[:, RD:RD + 7, :], T.tmc[:, 0:7, :], A.add, u, w)
+            u = ts(T.sm[:, M3:NM, :], T.sm[:, M3:NM, :], lane, 32.0 * UNIT, A.is_equal, A.mult, g_q)
+            c_id = spread(0, NM, u, s_i)
+    t_k = None
+    for c in range(BL):
+        t_k = mm(T.mis[:, c:NC:BL], T.sl_x[:, c, :], T.lsel[:], True, True, t, c_ls)
+    st["x32"] = act(T.x32[:], T.xs[:, 0:CUT], ACT.Copy, 0.0, 1.0, t_x0)
+    c_m2 = vcopy(T.zm[:, 15:143:16], T.hm[:], f_zero)
+    fill(T.run[:, 0:16], 0.0)
+    fill(T.ys[:], -4096.0)
 
-    st = {"lane": None, "wm": None, "mx": None, "za": z_a, "zb": ("dz", 16)}
+    def fills():
+        fill(T.n32[:], -1.0 / 32)
+        st["zero"] = fill(T.srt[:, 0:8], NEG)
 
-    def off_chip_of(src):
-        r = T.rank_of(src)
-        return [d for d in T.cores[r + 1:] if d not in topo.cores_of(src)]
+    def feeders(r):
+        return [r - 1] if FOLD and r and near(r - 1, r) else list(range(r))
+
+    def near(a, b):
+        return T.cores[a] in topo.cores_of(T.cores[b])
 
     def link(src, dst):
-        eng = topo.engines(src, dst)
-        offs = off_chip_of(src)
-        if dst in offs:
+        eng = topo.engines(T.cores[src], T.cores[dst])
+        if not near(src, dst):
             return eng
-        if offs:
-            eng = [e for e in eng if e not in topo.engines(src, offs[0])]
-        return eng[::2]
+        far = [d for d in range(src + 1, nranks) if not near(src, d)]
+        if far:
+            eng = [e for e in eng if e not in topo.engines(T.cores[src], T.cores[far[0]])]
+        return eng[::STEP[bool(far)]]
 
-    def arrivals(r):
-        return len(link(T.cores[r], core))
+    def landed(li, r):
+        return ("r%d%d" % (li, r), len(link(r, rank)))
 
-    def nothing(*a):
-        return None
+    def sort_pass(kind, dig, off, dep, twin, free, hook):
+        k = {}
 
-    def sort_pass(nd, dig, off, dep, ps_free, early_v, inter, hook2, hook1, fillers, late):
-        mm(T.acc[:, 256:256 + EV], T.i192[:], dig[:, 1:NC:2], True, False, dep, c_192)
-        t_po = mm(T.acc[:, 256:256 + EV], T.ident[:], T.cio[:, 1:NC:2], False, True, c_id, c_cio)
-        t_dl = act2(T.dl[:], dig, ACT.Copy, -float(MID), 1.0, dep)
-        t_sq = act2(T.sq[:], dig, ACT.Square, -float(MID), 1.0, dep)
-        v_oh, v_po = None, None
-        for d in range(nd):
-            if d == 4:
-                early_v()
-            if d == 12:
-                v_po = vcopy(T.poff[:], T.acc[:, 256:256 + EV], t_po)
-            v_oh = ts(T.oh[:, NC * d:NC * d + NC], dig, float(d), None, A.is_equal, None, dep)
-        f_v, f_s = NC * nd, F - NC * nd
-        n = f_s // 512 + (f_s % 512 > 0)
-        relu, s_oh = list(ps_free), None
-        for b in range(n):
-            o, w, c, t = 512 * (b % 3), min(512, f_s - 512 * b), 512 * b, None
-            while c < 512 * b + w:
-                i = c // NC
-                m = min(NC * (i + 1), 512 * b + w)
-                e, j = nd + i - MID, nd + i - ND_S
-                z, k = T.psa[:, o + c - 512 * b:o + m - 512 * b], c - NC * i
-                if e:
-                    mm(z, T.dgm[:, 128 * j:128 * j + 128], T.dl[:, k:k + m - c], True, False, t_dl, c_dg, relu[b % 3])
-                    mm(z, T.e2r[:, 128 * abs(e):128 * abs(e) + 128], T.ones[0:1, 0:m - c], False, False, f_end)
-                t = mm(z, T.ident[:], T.sq[:, k:k + m - c], e == 0, True, t_sq, c_id, relu[b % 3])
-                c = m
-            if b == n - 1:
-                inter()
-            s_oh = act2(T.oh[:, f_v + 512 * b:f_v + 512 * b + w], T.psa[:, o:o + w], ACT.Relu, 1.0, -1.0, t, f_end)
-            relu[b % 3] = s_oh
-        sc, c, tok = None, 0, {}
-        while c < F:
-            w = min(3072, (f_v if c < f_v else F) - c)
-            need("v", v_oh, sc, s_oh if c >= f_v else None)
-            init = -128.0 if c == 0 else T.ct[:, c:c + 1]
-            sc = done("v", V.tensor_tensor_scan(T.ct[:, c + 1:c + w + 1], T.oh[:, c:c + w], T.zero[:, 0:w], init, A.add, A.add))
-            c += w
-            tok[c] = sc
-        bank = list(relu)
+        def pairs():
+            for s in range(8):
+                c = NC * s
+                while c < NC * (s + 1):
+                    e = min(NC * (s + 1), 512 * (c // 512 + 1))
+                    k["df", c // 512] = mm(T.psa[:, c:e], C(DF + s), dig[:, c - NC * s:e - NC * s], True, True, dep, c_id, *free)
+                    c = e
+            mm(T.mis[:, NC:2 * NC], C(I384), dig[:, 0:NC], True, False, twin)
+            k["po"] = mm(T.mis[:, NC:2 * NC], C(ID), T.cmod[:], False, True, c_cm)
 
-        def early(b):
-            z, a = T.psa[:, 512 * (b % 3):512 * (b % 3) + 512], 1024 * b
-            mm(z, T.lm[:], T.oh[:, a:a + 1024:2], True, False, v_oh, s_oh if a + 1024 > f_v else None, c_lm, bank[b % 3])
+        def equal(b):
+            if b < nv:
+                k["eq", b] = ts(T.eq[:, 512 * b:512 * b + 512], T.psa[:, 512 * b:512 * b + 512], 0.0, None, A.is_equal, None, k["df", b])
 
-        for b in range(3):
-            early(b)
-        hook2()
-        need("s", v_oh, s_oh, v_po)
-        s_2 = done("s", S.activation(T.g2[:], T.oh[:].indirect(T.poff[:]), ACT.Copy))
-        need("s", sc)
-        s_1 = done("s", S.activation(T.g1[:], T.ct[:].indirect(T.poff[:]), ACT.Copy))
-        hook1()
-        red, d, t = [], 0, None
-        for b in range(6):
-            z, a = T.psa[:, 512 * (b % 3):512 * (b % 3) + 512], 1024 * b
-            if b > 2:
-                early(b)
-            t = tok[min(k for k in tok if k >= a + 1024)]
-            t = mm(z, T.bm[:], T.ct[:, a:a + 1024:2], False, True, t, c_b)
-            bank[b % 3] = tt(T.msk[:, 512 * b:512 * b + 512], z, T.oh[:, a:a + 1024:2], A.mult, t)
-            red.append(bank[b % 3])
-            if b == 2:
-                fillers(sc)
-                for q in range(16):
-                    mm(T.mis[:, 256:256 + EV], T.m2l[:, 128 * q:128 * q + 128], T.g2[:, q:16 * EV:16], q == 0, False, s_2, c_m2)
-            if b in (2, 4, 5):
-                while EV * (d + 1) <= 512 * (b - 1):
-                    mm(T.acc[:, 0:EV], T.ident[:], T.msk[:, EV * d:EV * d + EV], d == 0, False, red[b - 2])
-                    d += 1
-        t_o = None
-        for q in range(16):
-            t_o = mm(T.mis[:, 256:256 + EV], T.m2[:, 128 * q:128 * q + 128], T.g1[:, q:16 * EV:16], False, q == 15, s_1)
-        while d < ND:
-            t = mm(T.acc[:, 0:EV], T.ident[:], T.msk[:, EV * d:EV * d + EV], False, d == ND - 1, red[min(5, (EV * d + EV - 1) // 512)])
-            d += 1
-        late()
-        ts(off[:, 1:NC:2], T.mis[:, 256:256 + EV], 2048.0, None, A.add, None, t_o)
-        return ts(off[:, 0:NC:2], T.acc[:, 0:EV], 2048.0, None, A.add, None, t), sc, bank
+        def equal_s():
+            z = T.eq[:, 512 * nv:]
+            t = act(z, T.psa[:, 512 * nv:], ACT.Square, 0.0, 32.0, k["df", 2])
+            t = act(z, z, ACT.Relu, 1.0, -1.0, t)
+            for b in range(nv, 3):
+                k["eq", b] = t
 
-    def layer(li, src, src_toks, key_tok, out, piece_done):
-        v = vcopy(T.ki[:], T.mis[:, 0:NC], key_tok)
-        v_lo = ts(T.loi[:], T.ki[:], 31, None, A.bitwise_and, None, v)
-        v_d1 = vcopy(T.dig1[:], T.loi[:], v_lo)
-        kt, t_p, jt, pb, ko = {}, [], [None], [], []
+        nv = 3 - PAIR_S[kind]
+        if kind != "first":
+            pairs()
+        if kind == "hi":
+            equal_s()
+        first, t_w = 2, twin
+        if twin is None:
+            first, t_w = 4, ts(dig[:, NC:], dig[:, 0:NC], -1.0 / 32, None, A.add, None, dep)
+        for d in range(first):
+            ts(T.oh[:, d, :], dig[:, 0:NC], d / 32.0, None, A.is_equal, None, dep)
+            hook("digit%d" % d, k)
+        d = 0
+        for i, n in enumerate(GROUPS):
+            for e in range(max(d, first), d + n, W):
+                tv = ts(T.oh[:, e:e + W, :], dig[:], e / 32.0, None, A.is_equal, None, t_w)
+                hook("digit%d" % e, k)
+            for l in range(16):
+                t_tot = mm(T.acc[:, BL * d:BL * (d + n)], to_lane(T.zm, l), T.oh[:, d:d + n, BL * l:BL * l + BL], l == 0, l == 15,
+                           tv, c_m2, *free)
+            d += n
+            if kind == "first" and i == 1:
+                pairs()
+            hook("group%d" % i, k)
+            if kind == "lo" and i == 0:
+                equal_s()
+        v_po = vcopy(T.poff[:], T.mis[:, NC:2 * NC], k["po"])
+        equal(0)
+        v_run = scan(T.run[:, 1:NT + 1], T.acc[:, 0:NT], T.zero[:, 0:NT], 0.0, A.add, A.add, t_tot, st["zero"])
+        mm(T.acc[:, NT:NT + 32], C(GE), T.run[:, 0:NT:BL], True, False, v_run)
+        t = mm(T.acc[:, NT:NT + 32], C(LM), T.run[:, BL:NT + 1:BL], False, True)
+        if kind != "hi" and sends:
+            t = k["ends"] = mm(T.acc[:, NT + 32:NT + 64], C(BM), T.run[:, BL:NT + 1:BL], True, True)
+        hook("starts", k)
+        equal(1)
+        t = ts(T.ys[:, 0:NT:BL], T.acc[:, NT:NT + 32], -MIDP - 1.0, None, A.add, None, t)
+        hook("ys", k)
+        v_tab = k["tab"] = scan(T.tab[:], T.ys[:], T.acc[:, 0:NT], -4096.0, A.max, A.add, t)
+        equal(2)
 
-        def pack_keys():
-            a = ts(T.keyi[:], T.ki[:], 1023, None, A.bitwise_and, None, v)
-            b = ts(T.h16[:], T.ki[:], 992, None, A.bitwise_and, None, v)
-            kt["pk"] = tt(T.pk[:], T.keyi[:], T.h16[:], A.add, a, b)
-            kt["key"] = a
-
-        def row_bank(ps, b, c, with_src, *deps):
+        def gather(l0, l1):
             t = None
-            if with_src:
-                mm(ps[:, 512 * b:512 * b + 512], T.ident[:], src[:, c:c + 512], True, False, c_id, *(deps + tuple(src_toks)))
-            for q in range(16):
-                t = mm(ps[:, 512 * b + q:512 * b + 512:16], T.m3[:, 128 * q:128 * q + 128], T.pk[:, c // 16:c // 16 + 32],
-                       not with_src, q == 15 or not with_src, kt["pk"], c_m3, *deps)
+            if l0 >= lv:
+                for l in range(l0, l1):
+                    t = act(T.gb[:, NC * l:NC * l + NC], T.tab[:].indirect(T.poff[:, BL * l:BL * l + BL]), ACT.Copy, 0.0,
+                            T.lmk[:, l:l + 1], v_tab, v_po, c_lk)
+            elif st["mkb"] is None:
+                for l in range(l0, l1):
+                    t = ts(T.gb[:, NC * l:NC * l + NC], T.tab[:].indirect(T.poff[:, BL * l:BL * l + BL]), T.lmk[:, l:l + 1], None,
+                           A.mult, None, v_tab, v_po)
+            else:
+                t = tt(T.gb[:, NC * l0:NC * l1], T.tab[:].indirect(T.poff[:, BL * l0:BL * l1]), T.mkb[:, NC * l0:NC * l1], A.mult,
+                       v_tab, v_po, st["mkb"])
             return t
 
-        def pack_p(i, free):
-            pb.append(row_bank(T.psb, i % 3, 512 * i, True, free))
+        def wrap(l0, l1, *deps):
+            a, b, t = BL * l0, BL * l1, None
+            for q in range(16):
+                t = mm(T.mis[:, a:b], to_lane(T.zm, q), T.gb[:, 16 * a + q:16 * b:16], False, q == 15 and len(deps) == 2, *deps)
+            return t
 
-        def pack_s(i):
-            t_p.append(act2(T.packed[:, 512 * i:512 * i + 512], T.psb[:, 512 * (i % 3):512 * (i % 3) + 512], ACT.Copy, SHIFT, 1.0,
-                            pb[i], st["mx"]))
+        lv, l1, l2 = BLOCKS["ends" if kind == "hi" and sends else kind]
+        hook("table", k)
+        for s in range(8):
+            mm(T.mis[:, 0:NC], C(RD + s), T.eq[:, NC * s:NC * s + NC], s == 0, False, v_po, k["eq", NC * s // 512],
+               k["eq", (NC * s + NC - 1) // 512])
+        ga, gs = gather(0, l1), gather(l2, 16)
+        hook("mid", k)
+        gb, gt = gather(l1, lv), gather(lv, l2)
+        wrap(0, l1, ga)
+        wrap(l2, 16, gs)
+        t = wrap(l1, l2, gb, gt)
+        hook("tail", k)
+        k["off"] = ts(off[:], T.mis[:, 0:NC], MIDP, None, A.add, None, t)
+        hook("off", k)
+        return k
 
-        def packs_x():
+    def layer(li, src, src_toks, key_tok, out, piece_done):
+        shift = float(SHIFT + li * LIFT * HI)
+        v_ri = ts(T.ri[:], T.mis[:, 0:NC], -31.0 / 64, None, A.add, None, key_tok)
+        v_d1 = tt(T.dig1[:, 0:NC], T.mis[:, 0:NC], T.ri[:], A.subtract, v_ri)
+        kt, kc = {}, T["kc%d" % li]
+        hi, v_hi = T.ri, v_ri
+        if li:
+            hi, v_hi = T.hii, ts(T.hii[:], T.ri[:], 31, None, A.bitwise_and, None, v_ri)
+
+        def hook1(name, k):
+            if name == "digit3":
+                kt["kf"] = tt(T.kf[:], hi[:], T.dig1[:, 0:NC], A.add, v_hi)
+            if name == "digit8":
+                kt["ko"] = ts(T.koff[:], T.kf[:], 32.0, None, A.mult, None, kt["kf"])
+                kt["kr"] = sgat(T.krow[:], kc[:].indirect(T.koff[:, 0:SP_V]), ACT.Copy, kt["ko"], c_kc[li])
+                kt["pk"] = tt(T.pk[:], hi[:, SP_V:], T.kf[:, SP_V:], A.add)
             for i in range(3):
-                pack_p(i, None)
+                if name == PACK[li][i]:
+                    mm(T.psb[:, 512 * i:512 * i + 512], C(ID), src[:, CUT + 512 * i:CUT + 512 * i + 512], True, False, c_id, *src_toks)
+                    for q in range(16):
+                        kt["pb", i] = mm(T.psb[:, 512 * i + q:512 * i + 512:16], C(M3 + q), T.pk[:, 32 * i:32 * i + 32], False,
+                                         q == 15, kt["pk"])
+            if name in COPY[li]:
+                a, b = COPY[li][name]
+                kt["pa"] = act(T.packed[:, 512 * a:512 * b], T.psb[:, 512 * a:512 * b], ACT.Copy, shift, 1.0, kt["pb", b - 1])
+            if name == "group3" and li == 0:
+                fills()
+            if not sends:
+                return
+            if name == "ys":
+                kt["ji"] = ts(T.ji[:], T.acc[:, NT + 32:NT + 64], -1.0, 0.0, A.add, A.max, k["ends"])
+            if name == "table":
+                kt["cb"] = ts(T.cb[:], T.ji[:], 4, None, A.logical_shift_right, None, kt["ji"])
+            if name == "mid":
+                ts(T.jt[:], T.cb[:], 16.0, lane, A.mult, A.add, kt["cb"])
+                vcopy(T.cc[:, 0:32], T.cb[:])
+                kt["lb"] = ts(T.lb[:], T.cb[:], 1.0 / BL, -11.0 / 24, A.mult, A.add)
+            if name == "tail":
+                kt["mk"] = tt(T.mk[:], T.jt[:], T.acc[:, NT + 32:NT + 64], A.is_lt, kt["lb"])
+                kt["mkl"] = ts(T.mkl[:], T.lb[:], lane, -1.0, A.is_equal, A.mult)
+                kt["ju"] = ts(T.ju[:], T.lb[:], -float(BL), None, A.mult, None)
+            if name == "off":
+                kt["cc"] = tt(T.cc[:, 32:64], T.ju[:], T.cb[:], A.add, kt["ju"])
 
-        def packs_y():
-            for i in range(3):
-                pack_s(i)
-            pack_p(3, t_p[0])
-
-        def packs_z():
-            pack_s(3)
-
-        def packs_l():
-            for i in (4, 5):
-                pack_p(i, t_p[i - 3])
-                pack_s(i)
-
-        def fillers(sc):
-            if sends:
-                jt[0] = mm(T.mis[:, 0:32], T.bm[:], T.ct[:, NC:F + 1:NC], True, True, sc)
-            ko.append(vcopy(T.koff[:], T.keyi[:], kt["key"]))
-            if st["lane"] is None:
-                a = ts(T.li[:], T.pi[:], 15, None, A.bitwise_and, None, c_io)
-                a = vcopy(T.lane[:], T.li[:], a)
-                st["lane"] = ts(T.dq[:], T.ml[:], T.lane[:], None, A.is_equal, None, a)
-
-        g_b = low(T.pkb, st["mx"])
-        v_o1, _, psa_t = sort_pass(ND_V[0], T.dig1[:], T.off1, v_d1, [None] * 3, pack_keys, packs_x, packs_y, packs_z, fillers,
-                                   packs_l)
-        need("v", v_o1, st["za"], *t_p[:(16 * SP_V + 511) // 512])
-        v_s1 = done("v", V.tensor_copy(T.los[:].indirect(T.off1[:, 0:SP_V]), T.packed[:, 0:16 * SP_V]))
-        need("s", v_o1, st["zb"], *t_p)
-        s_s1 = done("s", S.activation(T.losb[:].indirect(T.off1[:, SP_V:NC]), T.packed[:, 16 * SP_V:], ACT.Silu))
-        pk_r = [None, None]
-
-        def key_mm(h, *deps):
-            for b in range(3):
-                pk_r[h] = row_bank((T.psa, T.psb)[h], b, 1536 * h + 512 * b, False, *deps)
-
-        def key_rows(h):
-            return act2(T.krow[:, 1536 * h:1536 * h + 1536], (T.psa, T.psb)[h][:], ACT.Copy, SHIFT, 1.0, pk_r[h])
-
-        key_mm(1, *t_p[3:6])
-        t_hi, v_j, sc_hi = None, None, 1.0 / (16.0 * HI)
+        k1 = sort_pass("lo" if li else "first", T.dig1, T.off1, v_d1, None, [st["mx"]], hook1)
+        v_o1 = k1["off"]
+        if li == 0:
+            vcopy(T.i32[:, 0:128], C(ID), c_id)
+            st["i32"] = ts(T.i32[:, 128:256], C(ID), -1.0, None, A.mult, None)
+        v_s1 = tt(T.los[:].indirect(T.off1[:, 0:SP_V]), T.krow[:], T.x32[:], A.add, v_o1, st["za"], kt["kr"], st["x32"])
+        s_s1 = sgat(T.losb[:].indirect(T.off1[:, SP_V:NC]), T.packed[:], ACT.Silu, v_o1, st["zb"], kt["pa"])
         if sends:
-            v_j = ts(T.ji[:], T.mis[:, 0:32], 2048.0, None, A.add, None, jt[0], v_o1)
+            for q in range(16):
+                t = mm(T.psb[:, 1024:1028], to_lane(T.zm, q), T.cc[:, q:64:16], q == 0, q == 15, kt["cc"], kt["pa"])
+            for i in range(32):
+                t_rep = mm(T.psb[:, 32 * i:32 * i + 32], C(ID), T.mkl[:], True, True, kt["mkl"])
+            for b in range(2):
+                ts(T.lst[:, b:64:2], T.hi192[:], T.psb[:, 1026 + b:1027 + b], 1.0 / 16, A.add, A.mult, t, c_hi)
+            kt["l"] = ts(T.ls2[:], T.psb[:, 1024:1026], 1.0 / 16, None, A.mult, None)
+        t_hi, sc_hi, lift = None, 1.0 / (512.0 * HI), -li * LIFT / 1024.0
         need("v", v_s1)
         need("s", s_s1)
-        t_da = ("da%d" % li, 16)
+        t_da = []
         for c in range(S_TOK - PC, -1, -PC):
-            e_a = ts(T.ext[:, c:c + PC], T.los[:, c:c + PC], sc_hi, None, A.mult, None)
-            e_b = act2(T.yo[:, c:c + PC], T.losb[:, c:c + PC], ACT.Copy, 0.0, sc_hi)
-            if c <= 16 * SC_V < c + PC:
+            e_a = ts(T.ext[:, c:c + PC], T.los[:, c:c + PC], sc_hi, lift, A.mult, A.add)
+            e_b = act(T.yo[:, c:c + PC], T.losb[:, c:c + PC], ACT.Copy, lift, sc_hi)
+            if 16 * SC_V < c + PC:
+                a, sem = max(c, 16 * SC_V), "da%d%d" % (li, len(t_da))
                 need("g", e_a, s_s1)
-                g.dma_start(T.los[:, 16 * SC_V:], T.losb[:, 16 * SC_V:], accum_op=A.add).then_inc(T.sem[t_da[0]], 16)
+                g.dma_start(T.los[:, a:c + PC], T.losb[:, a:c + PC], accum_op=A.add).then_inc(T.sem[sem], 16)
+                t_da.append((sem, 16))
             for last, x, t in ((False, T.ext, e_a), (True, T.yo, e_b)):
                 for q in range(16):
-                    t_hi = mm(T.mis[:, c // 16:(c + PC) // 16], T.m2[:, 128 * q:128 * q + 128], x[:, c + q:c + PC:16],
-                              q == 0 and not last, q == 15 and last, t, c_m2, v_j)
-        g_a = low(T.packed, v_s1, s_s1)
-        t_kr = [None, None]
-        t_mk = None
+                    t_hi = mm(T.mis[:, c // 16:(c + PC) // 16], to_lane(T.zm, q), x[:, c + q:c + PC:16],
+                              q == 0 and not last, q == 15 and last, t, v_o1)
+        if li == 0:
+            low(T.pka[:, ZB:], [[0, S_TOK - ZB]], 0)
+            st["zw"] = low(T.pkb[:], [[0, S_TOK]], 0)
+            c_kc.append(low(T.kc1[:], [[HI, 32], [UNIT, 32]], SHIFT + LIFT * HI))
         if sends:
-            v_q = ts(T.jq[:], T.ji[:], 15, None, A.bitwise_and, None, v_j)
-            v_c = ts(T.jc[:], T.ji[:], 4, None, A.logical_shift_right, None, v_j)
-            t_mk = ts(T.mkt[:], T.jq[:], T.lane[:], None, A.is_gt, None, v_q, st["lane"])
-            v = tt(T.jt[:], T.jc[:], T.dq[:], A.mult, v_c, st["lane"])
-            need("v", v)
-            for b in range(2):
-                v = done("v", V.tensor_reduce(T.cw[:, b:b + 1], T.jt[:, 16 * b:16 * b + 16], AxisListType.X, A.add))
-        v_d2 = ts(T.dig2[:], T.mis[:, 0:NC], MAGIC, MAGIC + 1.0, A.add, A.subtract, t_hi)
+            s_rep = act(T.mrep[:], T.psb[:, 0:1024], ACT.Copy, 0.0, 1.0, t_rep)
+        v_d2 = [ts(T.dig2[:, NC * r:NC * r + NC], T.mis[:, 0:NC], MAGIC, MAGIC + (r + 1.0) / 32, A.add, A.subtract, t_hi)
+                for r in range(W)]
 
-        def lists(sc):
-            if sends:
+        def hook2(name, k):
+            if not sends:
+                return
+            if name == "digit0":
+                kt["ds"] = tt(T.dsel[:], T.dig2[:, 0:NC].indirect(T.ls2[:]), T.mk[:], A.add, kt["l"])
+            if name == "group3":
                 for b in range(2):
-                    kt["l"] = ts(T.lst[:, b:64:2], T.hi192[:], T.cw[:, b:b + 1], None, A.add, None, v, c_io)
-
-        v_o2, v_ct, _ = sort_pass(ND_V[1], T.dig2[:], T.off2, v_d2, [None] * 3, nothing, nothing, nothing, nothing, lists, nothing)
-        t_e, p, ps_a = None, None, v_o2
-        if sends:
-            need("s", kt["l"], v_ct)
-            s_1 = done("s", S.activation(T.e1[:], T.ct[:].indirect(T.lst[:]), ACT.Copy))
-            s_2 = done("s", S.activation(T.e2[:], T.oh[:].indirect(T.lst[:]), ACT.Copy))
-            for q in range(16):
-                mm(T.mis[:, 0:64], T.m2[:, 128 * q:128 * q + 128], T.e1[:, q:1024:16], q == 0, False, s_1, v_o2)
+                    mm(T.psb[:, 512 * b:512 * b + 512], T.n32[:], T.hrow[:, 512 * b:512 * b + 512], True, False, s_rep, c_hi)
+                    for i in range(16):
+                        c = 512 * b + 32 * i
+                        kt["z", b] = mm(T.psb[:, c:c + 32], C(ID), T.dsel[:], False, i == 15, kt["ds"])
             for b in range(2):
-                mm(T.psa[:, 512 * b:512 * b + 512], T.ident[:], T.e2[:, 512 * b:512 * b + 512], True, False, s_2, v_o2)
-                for i in range(16):
-                    c = 512 * b + 32 * i
-                    p = mm(T.psa[:, c:c + 32], T.ident[:], T.mkt[:], False, i == 15, t_mk)
-        need("v", v_o2, g_a, v_s1, s_s1)
-        v = done("v", V.tensor_tensor(T.packed[:].indirect(T.off2[:, 0:SC_V]), T.los[:, 0:16 * SC_V], T.losb[:, 0:16 * SC_V], A.add))
-        need("s", v_o2, g_b, t_da)
-        s_w = done("s", S.activation(T.pkb[:].indirect(T.off2[:, SC_V:NC]), T.los[:, 16 * SC_V:], ACT.Silu))
+                if name == ("starts", "table")[b]:
+                    kt["e3"] = ts(T.e3[:, 512 * b:512 * b + 512], T.psb[:, 512 * b:512 * b + 512], 0.0, None, A.is_equal, None, kt["z", b])
+            if name == "tail":
+                kt["e1"] = tt(T.e1[:], T.tab[:].indirect(T.lst[:]), T.mrep[:], A.mult, k["tab"], s_rep)
+
+        k2 = sort_pass("hi", T.dig2, T.off2, v_d2[0], v_d2[1], [], hook2)
+        v_o2 = k2["off"]
+        s_3 = kt.get("e3")
         if sends:
-            s_3 = ps_a = act2(T.e3[:], T.psa[:, 0:1024], ACT.Relu, -1.0, 1.0, p)
-            for q in range(16):
-                t_e = mm(T.mis[:, 0:64], T.m2[:, 128 * q:128 * q + 128], T.e3[:, q:1024:16], False, q == 15, s_3)
-        key_mm(0, ps_a)
-        t_kr[1] = key_rows(1)
-        need("v", v, s_w)
-        v_mx = done("v", V.tensor_tensor_scan(T.srt[:, 8:], T.packed[:], T.pkb[:], NEG, A.max, A.max))
-        st["mx"] = v_mx
+            for i, e in enumerate((T.e1, T.e3)):
+                for q in range(16):
+                    t_e = mm(T.mis[:, 384:448], to_lane(T.zm, q), e[:, q:1024:16], i + q == 0, i + q == 16, kt["e1"], s_3, v_o2)
+        need("v", v_o2, st["zw"], v_s1, s_s1)
+        v = done("v", V.tensor_tensor(T.pka[:].indirect(T.off2[:, 0:SC_V]), T.los[:, 0:16 * SC_V], T.losb[:, 0:16 * SC_V], A.add))
+        s_w = sgat(T.pkb[:].indirect(T.off2[:, SC_V:NC]), T.los[:, 16 * SC_V:], ACT.Silu, v_o2, st["zw"], *t_da)
+        banks = []
+        for i, (ps, o) in enumerate(((T.acc, 0), (T.psa, 1024), (T.psb, 1024))):
+            c = CUT + 512 * i
+            n = min(512, S_TOK - c)
+            banks.append((ps[:, o:o + n], c, n))
+            mm(ps[:, o:o + n], C(ID), src[:, c:c + n], True, False, v_o2, *src_toks)
+            mm(ps[:, o:o + n], T.i32[:, 128:256], T.packed[:, c - CUT:c - CUT + n], False, False, st["i32"])
+        if sends:
+            v_e = ts(T.eoff[:], T.mis[:, 384:448], -1.0, MIDP + 8.0, A.mult, A.add, t_e)
+        v_mx = st["mx"] = scan(T.srt[:, 8:], T.pka[:], T.pkb[:], NEG, A.max, A.max, v, s_w)
         tl = T["tl%d" % li]
         if sends:
-            v_e = ts(T.eoff[:], T.mis[:, 0:64], 2055.0, None, A.add, None, t_e)
-            v_t = tt(tl[:], T.srt[:].indirect(T.eoff[:]), T.kc[:], A.subtract, v_mx, v_e, c_kc)
+            v_t = tt(tl[:], T.srt[:].indirect(T.eoff[:]), kc[:], A.subtract, v_mx, v_e, c_kc[li])
             need("g", v_t)
-            off_chip = off_chip_of(core)
-            on_chip = [d for d in T.cores[rank + 1:] if d not in off_chip]
             total = 0
-            for group in [c for c in (off_chip[:1], on_chip + off_chip[1:]) if c]:
+            to = [d for d in range(rank + 1, nranks) if rank in feeders(d)]
+            far = [d for d in to if not near(rank, d)]
+            for group in (to,) if FOLD else [c for c in (far[:1], [d for d in to if d not in far[:1]]) if c]:
                 trans = []
                 for d in group:
-                    eng = link(core, d)
+                    srcs = [tl[:]]
+                    if feeders(d) == [rank]:
+                        srcs += [T["ld%d%d" % (li, r)][:] for r in feeders(rank)]
+                        need("g", *[landed(li, r) for r in feeders(rank)])
+                    eng = link(rank, d)
                     total += len(eng)
-                    rid, pid = topo.addr(d, core)
+                    rid, pid = topo.addr(T.cores[d], core)
                     trans.append(RemoteDMATransfer(dst_ids=[DstId(rid=rid, pnc=pid)], dma_engine_mask=mask_of(eng),
-                                                   remote_sem=T.sem["r%d%d" % (li, rank)], srcs=[tl[:]],
-                                                   dsts=[T["ld%d%d" % (li, rank)][:]]))
+                                                   remote_sem=T.sem["r%d%d" % (li, rank)], srcs=srcs,
+                                                   dsts=[T["ld%d%d" % (li, rank)][:]], alu_op=2 if len(srcs) > 1 else 0))
                 g.remote_dma_fused(trans, local_sem=T.sem["lo%d" % li])
             st["lo%d" % li] = total
         if li == 0:
-            st["zb"] = low(T.losb, v_mx, c=0)
+            st["zb"] = low(T.losb[:], [[0, S_TOK]], 0, 0, v_mx)
         a = 64 if sends else 96
-        need("v", v_mx)
-        v_a = done("v", V.tensor_copy(T.los[:, 0:16 * a], T.srt[:, 8:].indirect(T.off2[:, 0:a])))
-        need("s", v_mx)
-        s_a = done("s", S.activation(T.los[:, 16 * a:], T.srt[:, 8:].indirect(T.off2[:, a:NC]), ACT.Copy))
-        t_kr[0] = key_rows(0)
-        if st["wm"] is None:
-            st["wm"] = act2(T.wm[:], T.m2[:], ACT.Copy, 0.0, T.wc[:], c_m2, t_w)
-        dst = T.yl if rank > 0 else out
-        ys = []
-        for c, e in ((CUT, S_TOK), (0, CUT)):
-            need("v", v_a, s_a, t_kr[1], t_kr[0] if c < 1536 else None)
-            ys.append(done("v", V.tensor_tensor(dst[:, c:e], T.los[:].indirect(T.off1[:, c // 16:e // 16]), T.krow[:, c:e], A.subtract)))
-            if rank == 0:
-                for i, j in ((CUT, STORE), (STORE, S_TOK)) if c else ((0, CUT),):
-                    piece_done(i, j, ys[-1])
-        if li == 0:
-            st["za"] = low(T.los, *ys, c=0)
-        if rank > 0:
-            parts, c = [], CUT
-            for ps, o in ((T.acc, 0), (T.psa, 1024), (T.psb, 1024)):
-                n = min(512, S_TOK - c)
-                t = mm(ps[:, o:o + n], T.ident[:], T.yl[:, c:c + n], True, True, ys[0], t_kr[0], t_kr[1])
-                parts.append((ps, o, c, n, t))
-                c += n
-            tin = T["ld%d0" % li]
-            v_in = ("r%d0" % li, arrivals(0))
-            merge = []
-            for r in range(1, rank):
-                ps = (T.psa, T.psb)[r % 2]
-                for b in range(2):
-                    t = mm(ps[:, 512 * b:512 * b + 512], T.ident[:], T["ld%d%d" % (li, r)][:, 512 * b:512 * b + 512], True, True,
-                           ("r%d%d" % (li, r), arrivals(r)), ps_a, t_kr[0])
-                merge.append(((T.ta, T.tb)[r % 2], ps, t))
-            for nxt, ps, t in merge:
-                v_in = tt(nxt[:], ps[:, 0:1024], tin[:], A.max, t, v_in)
-                tin = nxt
-            need("s", v_in, ko[0])
-            s_t = done("s", S.activation(T.ext[:, CUT:], tin[:].indirect(T.koff[:, CUT // 16:]), ACT.Copy))
-            piece_done(0, CUT, tt(out[:, 0:CUT], tin[:].indirect(T.koff[:, 0:CUT // 16]), T.yl[:, 0:CUT], A.max, v_in, ys[1], ko[0]))
-            for ps, o, c, n, t in parts:
-                v = tt(out[:, c:c + n], ps[:, o:o + n], T.ext[:, c:c + n], A.max, t, s_t)
-                if c + n == STORE:
-                    piece_done(CUT, STORE, v)
-            piece_done(STORE, S_TOK, v)
+        v_a = vcopy(T.los[:, 0:16 * a], T.srt[:, 8:].indirect(T.off2[:, 0:a]), v_mx)
+        s_a = sgat(T.los[:, 16 * a:], T.srt[:, 8:].indirect(T.off2[:, a:NC]), ACT.Copy, v_mx)
+        ins = feeders(rank)
 
-    hk = []
+        def to_psum():
+            for r in ins[1:]:
+                for b in range(2):
+                    kt["in", r] = mm((T.psa, T.psb)[r % 2][:, 512 * b:512 * b + 512], C(ID),
+                                     T["ld%d%d" % (li, r)][:, 512 * b:512 * b + 512], True, True, landed(li, r), s_3, v_o2)
+
+        if li:
+            to_psum()
+        y_a = tt((T.yl if rank else out)[:, 0:CUT], T.los[:].indirect(T.off1[:, 0:CUT // 16]), T.krow[:], A.subtract, v_a, s_a)
+        parts = []
+        for z, c, n in banks:
+            t = sgat(T.pg[:, c - CUT:c - CUT + n], T.los[:].indirect(T.off1[:, c // 16:(c + n) // 16]), ACT.Copy, v_a, s_a)
+            parts.append((z, c, n, mm(z, T.i32[:, 0:128], T.pg[:, c - CUT:c - CUT + n], False, True, t)))
+        if li == 0:
+            st["za"] = low(T.los[:], [[0, S_TOK]], 0, 0, y_a, t)
+            st["wm"] = ts(T.zw[:, 15:143:16], T.hm[:], T.wc[:], 1.0 / 32, A.mult, A.mult, t_w)
+            t = fill(T.ones[:], 1.0)
+            for l in range(LV if rank else 0):
+                st["mkb"] = ts(T.mkb[:, NC * l:NC * l + NC], T.ones[:], T.lmk[:, l:l + 1], None, A.mult, None, t)
+        if rank == 0:
+            for z, c, n, t in parts:
+                piece_done(c, c + n, act(out[:, c:c + n], z, ACT.Copy, 0.0, 1.0, t))
+            piece_done(0, CUT, y_a)
+        else:
+            tin, v_in = T["ld%d%d" % (li, ins[0])], landed(li, ins[0])
+            if li == 0:
+                to_psum()
+            for r in ins[1:]:
+                nxt = (T.ta, T.tb)[r % 2]
+                tin, v_in = nxt, tt(nxt[:], (T.psa, T.psb)[r % 2][:, 0:1024], tin[:], A.max, kt["in", r], v_in)
+            s_t = [sgat(T.ext[:, c:e], tin[:].indirect(T.koff[:, c // 16:e // 16]), ACT.Copy, v_in, kt["ko"])
+                   for c, e in ((CUT, STORE), (STORE, S_TOK))]
+            for c, e in ((0, CUT // 2), (CUT // 2, CUT)) if li else ((0, CUT),):
+                piece_done(c, e, tt(out[:, c:e], tin[:].indirect(T.koff[:, c // 16:e // 16]), T.yl[:, c:e], A.max, v_in, y_a, kt["ko"]))
+            for z, c, n, t in parts:
+                piece_done(c, c + n, tt(out[:, c:c + n], z, T.ext[:, c:c + n], A.max, t, s_t[c >= STORE]))
+
+    hk, last, stores = [], {}, []
 
     def hash_piece(c, e, tok):
         t = None
         for q in range(16):
-            t = mm(T.mis[:, c // 16:e // 16], T.wm[:, 128 * q:128 * q + 128], T.y1[:, c + q:e:16], q == 0, q == 15, tok, st["wm"])
+            t = mm(T.mis[:, c // 16:e // 16], to_lane(T.zw, q), T.y1[:, c + q:e:16], q == 0, q == 15, tok, st["wm"])
+        if c == 0:
+            st["x32"] = act(T.x32[:], T.y1[:, 0:CUT], ACT.Copy, 0.0, 1.0, tok)
         hk.append((tok, t))
 
-    def store_piece(c, e, tok):
-        dma("y", {0: "dy0", CUT: "dy1"}.get(c, "dy2"), T.y[:, c:e], T.yo[:, c:e], tok)
+    def joined(piece):
+        def f(c, e, tok):
+            if c == CUT:
+                last["tok"] = tok
+            elif e == STORE:
+                piece(CUT, STORE, tok)
+            else:
+                piece(c, e, tok)
+        return f
 
-    layer(0, T.xs, t_x, t_k, T.y1, hash_piece)
-    layer(1, T.y1, [h[0] for h in hk], max(h[1] for h in hk), T.yo, store_piece)
+    def store_piece(c, e, tok):
+        stores.append(dma("y", "dy%d" % len(stores), T.y[:, c:e], T.yo[:, c:e], tok))
+
+    layer(0, T.xs, [t_x], t_k, T.y1, joined(hash_piece))
+    layer(1, T.y1, [h[0] for h in hk], max(h[1] for h in hk), T.yo, joined(store_piece))
 
     for q in ("v", "s", "p", "g"):
         need("g", ("c" + q, count[q]))
-    for s in ("ds0", "ds1", "dx0", "dx1", "dw", "dz", "da0", "da1", "dy0", "dy1", "dy2"):
+    for s in LOCAL:
         need("g", (s, 16))
+    need("g", *stores)
     if sends:
         for li in range(2):
             need("g", ("lo%d" % li, st["lo%d" % li]))

@@ -3,36 +3,41 @@ from concourse.mybir import dt, AluOpType, AxisListType, ActivationFunctionType
 
 S_TOK, NC, ND, BL = 3072, 192, 32, 12
 NT = ND * BL
-UNIT = 510
+UNIT = 512
 HI = 64 * UNIT
 NEG = -1000000.0
 MAGIC = 393216.0
-SHIFT = 26440
-LIFT = 34
+SHIFT = 960
+LIFT = 32
 MIDP = 1536.0
 SP_V = 96
 PC = 1024
+PD = 2048
 SC_V = 98
 CUT = 16 * SP_V
 STORE = CUT + 1024
 BLOCKS = {"first": (9, 5, 12), "lo": (9, 5, 12), "hi": (9, 5, 12), "ends": (7, 5, 11)}
 LV = 9
-ZB = 1024
-FOLD, STEP = False, (2, 2)
+ZA = 1024
+ZB = 384
+STEP, DIRECT = (2, 1), (1, 0)
 W = 2
-GROUPS = (10, 8, 8, 6)
-PAIR_S = {"first": 0, "lo": 1, "hi": 2}
+EARLY = 16
+KF, KO = ("digit3", "digit6"), ("digit8", "digit10")
+GROUPS = {"first": (10, 8, 8, 6), "lo": (8, 8, 8, 8), "hi": (10, 8, 8, 6)}
+HOT_S = {"first": 0, "lo": 4, "hi": 0}
+PAIR_S = {"first": 1, "lo": 1, "hi": 2}
 DF, ID, I384, RD, LM, GE, BM, M3, NM = 0, 8, 9, 10, 18, 19, 20, 21, 37
-PACK = (("table", "table", "table"), ("group3", "starts", "table"))
+PACK = (("group3", "starts", "table"), ("group3", "starts", "table"))
 COPY = ({"tail": (0, 3)}, {"starts": (0, 1), "tail": (1, 3)})
 
 SB = {"bfloat16": {"xs": S_TOK, "y1": S_TOK, "yl": CUT, "yo": S_TOK, "ext": S_TOK, "ones": NC,
-                   "zero": NT, "dig1": W * NC, "dig2": W * NC, "cmod": NC, "eq": 1536, "run": NT + 16, "lsel": 16, "mkb": NC * LV,
+                   "zero": NT, "cmod": NC, "eq": 1536, "run": NT + 16, "cnt": NT, "lsel": 16, "mkb": NC * LV,
                    "mk": 32, "mkl": 32, "cc": 64, "dsel": 32, "mrep": 1024, "e3": 1024, "tl0": 1024, "tl1": 1024,
                    "ld00": 1024, "ld01": 1024, "ld02": 1024, "ld10": 1024, "ld11": 1024, "ld12": 1024, "ta": 1024, "tb": 1024},
-      "float32": {"wc": 1, "wc32": 1, "lane": 2, "one8": 8, "hm0": 8, "hm": 8, "lmk": 16, "hi192": 32, "kc0": 1024, "kc1": 1024,
-                  "jt": 32, "ju": 32, "ys": NT, "tab": NT, "packed": S_TOK - CUT, "pka": S_TOK, "pkb": S_TOK, "krow": CUT,
-                  "x32": CUT, "pg": S_TOK - CUT, "i32": 256, "los": S_TOK, "losb": S_TOK, "srt": S_TOK + 8},
+      "float32": {"wc": 1, "wc32": 1, "lane": 2, "one8": 8, "hm0": 8, "hm": 8, "lmk": 16, "hi192": 32, "kh": 1024, "kc": 1024,
+                  "jt": 32, "ju": 32, "tab": NT, "packed": S_TOK - CUT, "pka": S_TOK, "pkb": S_TOK, "krow": CUT,
+                  "x32": CUT, "pg": S_TOK - CUT, "i32": 256, "srt": S_TOK + 8},
       "int32": {"sl_i": NC, "pi": 1, "li": 1, "ri": NC, "hii": NC, "ji": 32, "cb": 32, "lb": 32},
       "float16": {"kf": NC, "pk": NC - SP_V, "gb": S_TOK, "e1": 1024},
       "uint16": {"koff": NC, "poff": NC, "off1": NC, "off2": NC, "eoff": 64, "lst": 64, "ls2": 2}}
@@ -44,16 +49,19 @@ SCRATCH = {
     "urow": ("sbuf", [128, 8, 16], "bfloat16"), "vrow": ("sbuf", [128, 8, 16], "int32"),
     "tma": ("sbuf", [128, 8, 16], "bfloat16"), "tmb": ("sbuf", [128, 8, 16], "bfloat16"),
     "tmc": ("sbuf", [128, 8, 16], "bfloat16"),
-    "hrow": ("sbuf", [1, 1024], "bfloat16"), "n32": ("sbuf", [1, 128], "bfloat16"),
+    "dig1": ("sbuf", [128, W, NC], "bfloat16"), "dig2": ("sbuf", [128, W, NC], "bfloat16"),
+    "lo": ("sbuf", [128, 2, S_TOK], "float32"), "exd": ("sbuf", [16, PD], "bfloat16"), "zs": ("sbuf", [16, 144], "bfloat16"),
+    "zt": ("sbuf", [16, 8], "bfloat16"), "lft": ("sbuf", [1, 256], "bfloat16"),
+    "ys": ("sbuf", [1, NT], "bfloat16"), "hrow": ("sbuf", [1, 1024], "bfloat16"), "n32": ("sbuf", [1, 128], "bfloat16"),
     "psa": ("psum", [128, 1536], "float32"), "psb": ("psum", [128, 1536], "float32"),
     "acc": ("psum", [128, 512], "float32"), "mis": ("psum", [128, 512], "float32"),
 }
 for _t in SB:
     for _n in SB[_t]:
         SCRATCH[_n] = ("sbuf", [128, SB[_t][_n]], _t)
-LOCAL = ["dx0", "dx1", "ds", "dw", "da00", "da01", "da10", "da11"]
-SEMAPHORES = (["cv", "cs", "cp", "cg", "lo0", "lo1", "dy0", "dy1", "dy2", "dy3"] + LOCAL
-              + ["r%d%d" % (a, b) for a in range(2) for b in range(3)])
+LOCAL = ["dx0", "dx1", "ds", "dw", "dz", "da00", "da01", "da10", "da11", "de0", "de1"]
+SEMAPHORES = (["cv", "cs", "cp", "cg", "lo0", "lo1", "dy0", "dy1", "dy2", "dy3", "dy4"] + LOCAL
+              + ["r%d%d%d" % (a, b, h) for a in range(2) for b in range(3) for h in range(2)])
 
 
 def mask_of(engines):
@@ -136,14 +144,18 @@ def rank_program(g, core, T, topo):
     def C(j):
         return T.cm[:, j, :]
 
+    def lo(w, a=0, b=S_TOK):
+        return T.lo[:, w, a:b]
+
     def to_lane(z, q):
         return z[:, 15 - q:143 - q]
 
     t_s = dma("y", "ds", T.sl_i[:], T.slot[:])
-    t_x0 = dma("y", "dx0", T.xs[:, 0:CUT], T.x[:, 0:CUT])
     t_x = dma("y", "dx1", T.xs[:, CUT:], T.x[:, CUT:])
     t_w = dma("y", "dw", T.wc[:], T.w[:])
 
+    fill(T.zs[:], 0.0)
+    fill(T.zt[:], 1.0 / (32.0 * HI))
     f_8 = fill(T.one8[:], 1.0)
     fill(T.zm[:], 0.0)
     fill(T.zw[:], 0.0)
@@ -158,13 +170,17 @@ def rank_program(g, core, T, topo):
     g_r = sel(T.row1[:], T.mrow[:], [[-1, 8], [-1, 16]], A.is_ge, -1.0, 14, 0, g_m)
     g_q = low(T.sm[:, M3:NM, :], [[1, 16], [0, 16]], 0)
     st = {"wm": None, "mkb": None, "mx": None}
-    c_kc = [low(T.kc0[:], [[HI, 32], [UNIT, 32]], SHIFT)]
+    c_kh = low(T.kh[:], [[HI // 2, 32], [UNIT // 2, 32]], SHIFT // 2)
     c_cm = low(T.cmod[:], [[0, 16], [1, BL]], 0)
-    st["za"] = low(T.los[:], [[0, S_TOK]], 0)
-    st["zb"] = low(T.losb[:], [[0, S_TOK]], 0)
+    st["x32"] = dma("g", "dx0", T.x32[:], T.x[:, 0:CUT])
+    t = low(lo(0, 0, ZA), [[0, ZA]], 0)
+    t_z = dma("y", "dz", lo(1, 0, ZA), lo(0, 0, ZA), t)
+    st["za"] = low(lo(0, ZA), [[0, S_TOK - ZA]], 0)
+    st["zb"] = low(lo(1, ZA), [[0, S_TOK - ZA]], 0)
+    t = sel(T.zt[:], T.zt[:], [[-2, 8]], A.is_ge, 0.0, 0, 1)
+    c_zs = sel(T.zs[:, 15:143:16], T.zt[:], [[2, 8]], A.is_ge, 0.0, 1, -1, t)
     low(T.hi192[:], [[NC, 32]], 0)
     c_hi = low(T.hrow[:], [[1, 32], [0, 32]], 0)
-    low(T.pka[:, 0:ZB], [[0, ZB]], 0)
 
     def spread(j0, j1, *deps):
         t = None
@@ -186,29 +202,34 @@ def rank_program(g, core, T, topo):
     c_lk = ts(T.lmk[:], T.mrow[:, 0, :], lane, None, A.is_equal, None)
     v_b = ts(T.tmb[:], T.vrow[:], lane, None, A.is_equal, None, v_v)
     v0 = vcopy(T.sl_h[:], T.sl_i[:], t_s)
-    u = ts(T.tmc[:], T.urow[:], T.lane[:, 1:2], -1.0, A.is_equal, A.mult, g_u, v_l2)
-    w = ts(T.sm[:, RD:RD + 8, :], T.row1[:], lane, -1.0, A.is_equal, A.mult, g_r)
-    tt(T.sm[:, DF:DF + 8, :], T.tma[:], T.tmb[:], A.subtract, v_b)
+    t = tt(T.sm[:, DF:DF + 8, :], T.tma[:], T.tmb[:], A.subtract, v_b)
+    c_id = spread(0, RD, t, s_i)
     for h in range(8):
         t = ts(T.sl_x[:, :, 16 * h:16 * h + 16], T.sl_h[:], T.hm[:, h:h + 1], None, A.mult, None, v0, c_hm)
-        if h == 2:
-            tt(T.sm[:, RD:RD + 7, :], T.sm[:, RD:RD + 7, :], T.tmc[:, 0:7, :], A.add, u, w)
-            u = ts(T.sm[:, M3:NM, :], T.sm[:, M3:NM, :], lane, 32.0 * UNIT, A.is_equal, A.mult, g_q)
-            c_id = spread(0, NM, u, s_i)
     t_k = None
     for c in range(BL):
         t_k = mm(T.mis[:, c:NC:BL], T.sl_x[:, c, :], T.lsel[:], True, True, t, c_ls)
-    st["x32"] = act(T.x32[:], T.xs[:, 0:CUT], ACT.Copy, 0.0, 1.0, t_x0)
+    u = ts(T.tmc[:], T.urow[:], T.lane[:, 1:2], -1.0, A.is_equal, A.mult, g_u, v_l2)
+    w = ts(T.sm[:, RD:RD + 8, :], T.row1[:], lane, -1.0, A.is_equal, A.mult, g_r)
+    ts(T.sm[:, M3:NM, :], T.sm[:, M3:NM, :], lane, 32.0 * UNIT, A.is_equal, A.mult, g_q)
     c_m2 = vcopy(T.zm[:, 15:143:16], T.hm[:], f_zero)
     fill(T.run[:, 0:16], 0.0)
-    fill(T.ys[:], -4096.0)
+    t = tt(T.sm[:, RD:RD + 7, :], T.sm[:, RD:RD + 7, :], T.tmc[:, 0:7, :], A.add, u, w)
+    st["rd"] = spread(RD, NM, t)
 
-    def fills():
+    def fills(i):
+        if i == 0:
+            fill(T.ones[:], 1.0)
+            st["ys"] = fill(T.ys[:], -4096.0)
+            return
+        need("v", st["ys"])
+        fill(T.ys[:, 0:NT:BL], -MIDP)
         fill(T.n32[:], -1.0 / 32)
         st["zero"] = fill(T.srt[:, 0:8], NEG)
 
-    def feeders(r):
-        return [r - 1] if FOLD and r and near(r - 1, r) else list(range(r))
+    def first_to(li, r):
+        far = [d for d in range(r + 1, nranks) if not near(r, d)]
+        return far[-li] if far else r + 1
 
     def near(a, b):
         return T.cores[a] in topo.cores_of(T.cores[b])
@@ -222,21 +243,22 @@ def rank_program(g, core, T, topo):
             eng = [e for e in eng if e not in topo.engines(T.cores[src], T.cores[far[0]])]
         return eng[::STEP[bool(far)]]
 
-    def landed(li, r):
-        return ("r%d%d" % (li, r), len(link(r, rank)))
+    def landed(li, r, h):
+        return ("r%d%d%d" % (li, r, h), len(link(r, rank)))
 
-    def sort_pass(kind, dig, off, dep, twin, free, hook):
+    def sort_pass(kind, dig, off, dep, late, free, hook):
         k = {}
 
-        def pairs():
+        def pairs(a, b, tok):
             for s in range(8):
-                c = NC * s
-                while c < NC * (s + 1):
-                    e = min(NC * (s + 1), 512 * (c // 512 + 1))
-                    k["df", c // 512] = mm(T.psa[:, c:e], C(DF + s), dig[:, c - NC * s:e - NC * s], True, True, dep, c_id, *free)
+                c = NC * s + a
+                while c < NC * s + b:
+                    e = min(NC * s + b, 512 * (c // 512 + 1))
+                    k["df", c // 512] = mm(T.psa[:, c:e], C(DF + s), dig[:, 0, c - NC * s:e - NC * s], True, True, tok, c_id, *free)
                     c = e
-            mm(T.mis[:, NC:2 * NC], C(I384), dig[:, 0:NC], True, False, twin)
-            k["po"] = mm(T.mis[:, NC:2 * NC], C(ID), T.cmod[:], False, True, c_cm)
+            if a == 0:
+                mm(T.mis[:, NC:2 * NC], C(I384), dig[:, 0, :], True, False)
+                k["po"] = mm(T.mis[:, NC:2 * NC], C(ID), T.cmod[:], False, True, c_cm)
 
         def equal(b):
             if b < nv:
@@ -249,43 +271,56 @@ def rank_program(g, core, T, topo):
             for b in range(nv, 3):
                 k["eq", b] = t
 
-        nv = 3 - PAIR_S[kind]
-        if kind != "first":
-            pairs()
-        if kind == "hi":
+        nv, s_oh = 3 - PAIR_S[kind], None
+        if late is None:
+            pairs(0, NC, dep)
+            first, t_w = 4, ts(dig[:, 1, :], dig[:, 0, :], -1.0 / 32, None, A.add, None, dep)
+            for e in range(ND - HOT_S[kind], ND, W):
+                s_oh = act(T.oh[:, e:e + W, :], dig[:], ACT.Square, -float(e), 32.0, t_w)
+            if HOT_S[kind]:
+                z = T.oh[:, ND - HOT_S[kind]:, :]
+                s_oh = act(z, z, ACT.Relu, 1.0, -1.0, s_oh)
+            for d in range(first):
+                ts(T.oh[:, d, :], dig[:, 0, :], d / 32.0, None, A.is_equal, None)
+                hook("digit%d" % d, k)
+        else:
+            first, (n, wrapped, make) = EARLY, late
+            t_w = wrapped()
+            pairs(n, NC, dep)
+            for d in range(0, first, W):
+                if d == first - 2 * W:
+                    t_w = make(t_w)
+                ts(T.oh[:, d:d + W, n:], dig[:, :, n:], d / 32.0, None, A.is_equal, None, dep)
+            pairs(0, n, t_w)
             equal_s()
-        first, t_w = 2, twin
-        if twin is None:
-            first, t_w = 4, ts(dig[:, NC:], dig[:, 0:NC], -1.0 / 32, None, A.add, None, dep)
-        for d in range(first):
-            ts(T.oh[:, d, :], dig[:, 0:NC], d / 32.0, None, A.is_equal, None, dep)
-            hook("digit%d" % d, k)
         d = 0
-        for i, n in enumerate(GROUPS):
-            for e in range(max(d, first), d + n, W):
-                tv = ts(T.oh[:, e:e + W, :], dig[:], e / 32.0, None, A.is_equal, None, t_w)
-                hook("digit%d" % e, k)
+        for i, n in enumerate(GROUPS[kind]):
+            for e in range(d, min(d + n, ND - HOT_S[kind]), W):
+                if e >= first:
+                    tv = ts(T.oh[:, e:e + W, :], dig[:], e / 32.0, None, A.is_equal, None, t_w)
+                    hook("digit%d" % e, k)
+                elif late:
+                    tv = ts(T.oh[:, e:e + W, 0:late[0]], dig[:, :, 0:late[0]], e / 32.0, None, A.is_equal, None, t_w)
             for l in range(16):
                 t_tot = mm(T.acc[:, BL * d:BL * (d + n)], to_lane(T.zm, l), T.oh[:, d:d + n, BL * l:BL * l + BL], l == 0, l == 15,
-                           tv, c_m2, *free)
+                           tv, c_m2, s_oh if d + n > ND - HOT_S[kind] else None, *free)
             d += n
-            if kind == "first" and i == 1:
-                pairs()
+            if i == 3:
+                mm(T.psb[:, 1024:1024 + NT], T.ones[0:1, 0:128], T.ys[:], True, False, st["zero"])
             hook("group%d" % i, k)
-            if kind == "lo" and i == 0:
+            if kind != "hi" and i == 1:
                 equal_s()
         v_po = vcopy(T.poff[:], T.mis[:, NC:2 * NC], k["po"])
         equal(0)
         v_run = scan(T.run[:, 1:NT + 1], T.acc[:, 0:NT], T.zero[:, 0:NT], 0.0, A.add, A.add, t_tot, st["zero"])
-        mm(T.acc[:, NT:NT + 32], C(GE), T.run[:, 0:NT:BL], True, False, v_run)
-        t = mm(T.acc[:, NT:NT + 32], C(LM), T.run[:, BL:NT + 1:BL], False, True)
+        v_cnt = vcopy(T.cnt[:], T.acc[:, 0:NT])
+        mm(T.psb[:, 1024:1024 + NT:BL], C(GE), T.run[:, 0:NT:BL], False, False, v_run, st["rd"])
+        t = mm(T.psb[:, 1024:1024 + NT:BL], C(LM), T.run[:, BL:NT + 1:BL], False, True)
         if kind != "hi" and sends:
-            t = k["ends"] = mm(T.acc[:, NT + 32:NT + 64], C(BM), T.run[:, BL:NT + 1:BL], True, True)
+            k["ends"] = mm(T.acc[:, NT + 32:NT + 64], C(BM), T.run[:, BL:NT + 1:BL], True, True, v_cnt)
         hook("starts", k)
         equal(1)
-        t = ts(T.ys[:, 0:NT:BL], T.acc[:, NT:NT + 32], -MIDP - 1.0, None, A.add, None, t)
-        hook("ys", k)
-        v_tab = k["tab"] = scan(T.tab[:], T.ys[:], T.acc[:, 0:NT], -4096.0, A.max, A.add, t)
+        v_tab = k["tab"] = scan(T.tab[:], T.psb[:, 1024:1024 + NT], T.cnt[:], -4096.0, A.max, A.add, t, v_cnt)
         equal(2)
 
         def gather(l0, l1):
@@ -321,49 +356,54 @@ def rank_program(g, core, T, topo):
         wrap(l2, 16, gs)
         t = wrap(l1, l2, gb, gt)
         hook("tail", k)
-        k["off"] = ts(off[:], T.mis[:, 0:NC], MIDP, None, A.add, None, t)
+        k["off"] = ts(off[:], T.mis[:, 0:NC], MIDP - 1.0, None, A.add, None, t)
         hook("off", k)
         return k
 
     def layer(li, src, src_toks, key_tok, out, piece_done):
         shift = float(SHIFT + li * LIFT * HI)
         v_ri = ts(T.ri[:], T.mis[:, 0:NC], -31.0 / 64, None, A.add, None, key_tok)
-        v_d1 = tt(T.dig1[:, 0:NC], T.mis[:, 0:NC], T.ri[:], A.subtract, v_ri)
-        kt, kc = {}, T["kc%d" % li]
+        if li == 0:
+            fills(0)
+        v_d1 = tt(T.dig1[:, 0, :], T.mis[:, 0:NC], T.ri[:], A.subtract, v_ri)
+        kt = {}
         hi, v_hi = T.ri, v_ri
         if li:
             hi, v_hi = T.hii, ts(T.hii[:], T.ri[:], 31, None, A.bitwise_and, None, v_ri)
 
         def hook1(name, k):
-            if name == "digit3":
-                kt["kf"] = tt(T.kf[:], hi[:], T.dig1[:, 0:NC], A.add, v_hi)
-            if name == "digit8":
+            if name == KF[li]:
+                kt["kf"] = tt(T.kf[:], hi[:], T.dig1[:, 0, :], A.add, v_hi)
+            if name == KO[li]:
                 kt["ko"] = ts(T.koff[:], T.kf[:], 32.0, None, A.mult, None, kt["kf"])
-                kt["kr"] = sgat(T.krow[:], kc[:].indirect(T.koff[:, 0:SP_V]), ACT.Copy, kt["ko"], c_kc[li])
+                kt["kr"] = act(T.krow[:], T.kh[:].indirect(T.koff[:, 0:SP_V]), ACT.Copy, shift - SHIFT, 2.0, kt["ko"], c_kh)
                 kt["pk"] = tt(T.pk[:], hi[:, SP_V:], T.kf[:, SP_V:], A.add)
             for i in range(3):
                 if name == PACK[li][i]:
-                    mm(T.psb[:, 512 * i:512 * i + 512], C(ID), src[:, CUT + 512 * i:CUT + 512 * i + 512], True, False, c_id, *src_toks)
+                    mm(T.psb[:, 512 * i:512 * i + 512], C(ID), src[:, CUT + 512 * i:CUT + 512 * i + 512], True, False, st["rd"],
+                       k.get("tab"), *src_toks)
                     for q in range(16):
                         kt["pb", i] = mm(T.psb[:, 512 * i + q:512 * i + 512:16], C(M3 + q), T.pk[:, 32 * i:32 * i + 32], False,
                                          q == 15, kt["pk"])
             if name in COPY[li]:
                 a, b = COPY[li][name]
                 kt["pa"] = act(T.packed[:, 512 * a:512 * b], T.psb[:, 512 * a:512 * b], ACT.Copy, shift, 1.0, kt["pb", b - 1])
-            if name == "group3" and li == 0:
-                fills()
+            if name == "digit3" and li == 0:
+                fills(1)
+            if name == "tail" and li == 0:
+                for i in range(2):
+                    fill(T.lft[:, 128 * i:128 * i + 128], i * LIFT + 0.25)
             if not sends:
                 return
-            if name == "ys":
-                kt["ji"] = ts(T.ji[:], T.acc[:, NT + 32:NT + 64], -1.0, 0.0, A.add, A.max, k["ends"])
             if name == "table":
-                kt["cb"] = ts(T.cb[:], T.ji[:], 4, None, A.logical_shift_right, None, kt["ji"])
+                kt["ji"] = ts(T.ji[:], T.acc[:, NT + 32:NT + 64], -1.0, 0.0, A.add, A.max, k["ends"])
             if name == "mid":
+                kt["cb"] = ts(T.cb[:], T.ji[:], 4, None, A.logical_shift_right, None, kt["ji"])
+            if name == "tail":
                 ts(T.jt[:], T.cb[:], 16.0, lane, A.mult, A.add, kt["cb"])
                 vcopy(T.cc[:, 0:32], T.cb[:])
-                kt["lb"] = ts(T.lb[:], T.cb[:], 1.0 / BL, -11.0 / 24, A.mult, A.add)
-            if name == "tail":
-                kt["mk"] = tt(T.mk[:], T.jt[:], T.acc[:, NT + 32:NT + 64], A.is_lt, kt["lb"])
+                t = ts(T.lb[:], T.cb[:], 1.0 / BL, -11.0 / 24, A.mult, A.add)
+                kt["mk"] = tt(T.mk[:], T.jt[:], T.acc[:, NT + 32:NT + 64], A.is_lt, t)
                 kt["mkl"] = ts(T.mkl[:], T.lb[:], lane, -1.0, A.is_equal, A.mult)
                 kt["ju"] = ts(T.ju[:], T.lb[:], -float(BL), None, A.mult, None)
             if name == "off":
@@ -374,8 +414,8 @@ def rank_program(g, core, T, topo):
         if li == 0:
             vcopy(T.i32[:, 0:128], C(ID), c_id)
             st["i32"] = ts(T.i32[:, 128:256], C(ID), -1.0, None, A.mult, None)
-        v_s1 = tt(T.los[:].indirect(T.off1[:, 0:SP_V]), T.krow[:], T.x32[:], A.add, v_o1, st["za"], kt["kr"], st["x32"])
-        s_s1 = sgat(T.losb[:].indirect(T.off1[:, SP_V:NC]), T.packed[:], ACT.Silu, v_o1, st["zb"], kt["pa"])
+        v_s1 = tt(lo(0).indirect(T.off1[:, 0:SP_V]), T.krow[:], T.x32[:], A.add, v_o1, st["za"], kt["kr"], st["x32"], t_z)
+        s_s1 = sgat(lo(1).indirect(T.off1[:, SP_V:NC]), T.packed[:], ACT.Silu, v_o1, st["zb"], kt["pa"], t_z)
         if sends:
             for q in range(16):
                 t = mm(T.psb[:, 1024:1028], to_lane(T.zm, q), T.cc[:, q:64:16], q == 0, q == 15, kt["cc"], kt["pa"])
@@ -384,58 +424,73 @@ def rank_program(g, core, T, topo):
             for b in range(2):
                 ts(T.lst[:, b:64:2], T.hi192[:], T.psb[:, 1026 + b:1027 + b], 1.0 / 16, A.add, A.mult, t, c_hi)
             kt["l"] = ts(T.ls2[:], T.psb[:, 1024:1026], 1.0 / 16, None, A.mult, None)
-        t_hi, sc_hi, lift = None, 1.0 / (512.0 * HI), -li * LIFT / 1024.0
+        t_dm = dma("g", "de%d" % li, T.exd[:], T.lo[0:128:16, :, 0:PD], v_s1, s_s1)
+        t_hi, t_ea, sc_hi, lift = {}, [], 1.0 / (512.0 * HI), -(li * LIFT + 0.25) / 1024.0
         need("v", v_s1)
         need("s", s_s1)
-        t_da = []
-        for c in range(S_TOK - PC, -1, -PC):
-            e_a = ts(T.ext[:, c:c + PC], T.los[:, c:c + PC], sc_hi, lift, A.mult, A.add)
-            e_b = act(T.yo[:, c:c + PC], T.losb[:, c:c + PC], ACT.Copy, lift, sc_hi)
-            if 16 * SC_V < c + PC:
-                a, sem = max(c, 16 * SC_V), "da%d%d" % (li, len(t_da))
-                need("g", e_a, s_s1)
-                g.dma_start(T.los[:, a:c + PC], T.losb[:, a:c + PC], accum_op=A.add).then_inc(T.sem[sem], 16)
-                t_da.append((sem, 16))
+        for c in range(S_TOK - PC, PD - 1, -PC):
+            e_a = ts(T.ext[:, c:c + PC], lo(0, c, c + PC), sc_hi, lift, A.mult, A.add)
+            t_ea.append(e_a)
+            e_b = act(T.yo[:, c:c + PC], lo(1, c, c + PC), ACT.Copy, lift, sc_hi)
             for last, x, t in ((False, T.ext, e_a), (True, T.yo, e_b)):
                 for q in range(16):
-                    t_hi = mm(T.mis[:, c // 16:(c + PC) // 16], to_lane(T.zm, q), x[:, c + q:c + PC:16],
-                              q == 0 and not last, q == 15 and last, t, v_o1)
+                    t_hi[c] = mm(T.mis[:, c // 16:(c + PC) // 16], to_lane(T.zm, q), x[:, c + q:c + PC:16],
+                                 q == 0 and not last, q == 15 and last, t, v_o1)
+
+        def late():
+            mm(T.acc[:, 0:PD // 16], T.n32[:], T.lft[:, 128 * li:128 * li + PD // 16], True, False, v_o1)
+            for q in range(16):
+                t = mm(T.acc[:, 0:PD // 16], to_lane(T.zs, q), T.exd[:, q:PD:16], False, q == 15, t_dm, c_zs)
+            return t
+
+        t_da = []
+        for a, b, t in ((S_TOK - PC, S_TOK, t_ea[0]), (16 * SC_V, S_TOK - PC, t_dm if PD > 16 * SC_V else t_ea[1])):
+            if li == 0:
+                z = ZB * len(t_da)
+                low(T.pka[:, z:z + ZB], [[0, ZB]], 0)
+            need("g", t)
+            g.dma_start(lo(0, a, b), lo(1, a, b), accum_op=A.add).then_inc(T.sem["da%d%d" % (li, len(t_da))], 16)
+            t_da.append(("da%d%d" % (li, len(t_da)), 16))
         if li == 0:
-            low(T.pka[:, ZB:], [[0, S_TOK - ZB]], 0)
+            low(T.pka[:, 2 * ZB:], [[0, S_TOK - 2 * ZB]], 0)
             st["zw"] = low(T.pkb[:], [[0, S_TOK]], 0)
-            c_kc.append(low(T.kc1[:], [[HI, 32], [UNIT, 32]], SHIFT + LIFT * HI))
         if sends:
             s_rep = act(T.mrep[:], T.psb[:, 0:1024], ACT.Copy, 0.0, 1.0, t_rep)
-        v_d2 = [ts(T.dig2[:, NC * r:NC * r + NC], T.mis[:, 0:NC], MAGIC, MAGIC + (r + 1.0) / 32, A.add, A.subtract, t_hi)
-                for r in range(W)]
+            s_kc = act(T.kc[:], T.kh[:], ACT.Copy, shift - SHIFT, 2.0, st["mx"])
+
+        def rounded(ps, a, b, tok):
+            return [ts(T.dig2[:, r, a:b], ps[:, a:b], MAGIC, MAGIC + r / 32.0, A.add, A.subtract, tok) for r in range(W)]
 
         def hook2(name, k):
             if not sends:
                 return
-            if name == "digit0":
-                kt["ds"] = tt(T.dsel[:], T.dig2[:, 0:NC].indirect(T.ls2[:]), T.mk[:], A.add, kt["l"])
+            if name == "group0":
+                kt["ds"] = tt(T.dsel[:], T.dig2[:, 0, :].indirect(T.ls2[:]), T.mk[:], A.add, kt["l"])
             if name == "group3":
-                for b in range(2):
+                for b in (1, 0):
                     mm(T.psb[:, 512 * b:512 * b + 512], T.n32[:], T.hrow[:, 512 * b:512 * b + 512], True, False, s_rep, c_hi)
                     for i in range(16):
                         c = 512 * b + 32 * i
                         kt["z", b] = mm(T.psb[:, c:c + 32], C(ID), T.dsel[:], False, i == 15, kt["ds"])
-            for b in range(2):
-                if name == ("starts", "table")[b]:
-                    kt["e3"] = ts(T.e3[:, 512 * b:512 * b + 512], T.psb[:, 512 * b:512 * b + 512], 0.0, None, A.is_equal, None, kt["z", b])
+                t = act(T.e3[:, 512:], T.psb[:, 512:1024], ACT.Square, 0.0, 32.0, kt["z", 1])
+                kt["e2"] = act(T.e3[:, 512:], T.e3[:, 512:], ACT.Relu, 1.0, -1.0, t)
+            if name == "table":
+                kt["e3"] = ts(T.e3[:, 0:512], T.psb[:, 0:512], 0.0, None, A.is_equal, None, kt["z", 0])
             if name == "tail":
                 kt["e1"] = tt(T.e1[:], T.tab[:].indirect(T.lst[:]), T.mrep[:], A.mult, k["tab"], s_rep)
 
-        k2 = sort_pass("hi", T.dig2, T.off2, v_d2[0], v_d2[1], [], hook2)
+        n = PD // 16
+        k2 = sort_pass("hi", T.dig2, T.off2, rounded(T.mis, n, NC, t_hi[PD])[1], (n, late, lambda t: rounded(T.acc, 0, n, t)[1]),
+                       [], hook2)
         v_o2 = k2["off"]
-        s_3 = kt.get("e3")
+        s_3 = kt.get("e2")
         if sends:
             for i, e in enumerate((T.e1, T.e3)):
                 for q in range(16):
-                    t_e = mm(T.mis[:, 384:448], to_lane(T.zm, q), e[:, q:1024:16], i + q == 0, i + q == 16, kt["e1"], s_3, v_o2)
+                    t_e = mm(T.mis[:, 384:448], to_lane(T.zm, q), e[:, q:1024:16], i + q == 0, i + q == 16, kt["e1"], kt["e2"], v_o2)
         need("v", v_o2, st["zw"], v_s1, s_s1)
-        v = done("v", V.tensor_tensor(T.pka[:].indirect(T.off2[:, 0:SC_V]), T.los[:, 0:16 * SC_V], T.losb[:, 0:16 * SC_V], A.add))
-        s_w = sgat(T.pkb[:].indirect(T.off2[:, SC_V:NC]), T.los[:, 16 * SC_V:], ACT.Silu, v_o2, st["zw"], *t_da)
+        v = done("v", V.tensor_tensor(T.pka[:].indirect(T.off2[:, 0:SC_V]), lo(0, 0, 16 * SC_V), lo(1, 0, 16 * SC_V), A.add))
+        s_w = sgat(T.pkb[:].indirect(T.off2[:, SC_V:NC]), lo(0, 16 * SC_V), ACT.Silu, v_o2, st["zw"], *t_da)
         banks = []
         for i, (ps, o) in enumerate(((T.acc, 0), (T.psa, 1024), (T.psb, 1024))):
             c = CUT + 512 * i
@@ -444,71 +499,82 @@ def rank_program(g, core, T, topo):
             mm(ps[:, o:o + n], C(ID), src[:, c:c + n], True, False, v_o2, *src_toks)
             mm(ps[:, o:o + n], T.i32[:, 128:256], T.packed[:, c - CUT:c - CUT + n], False, False, st["i32"])
         if sends:
-            v_e = ts(T.eoff[:], T.mis[:, 384:448], -1.0, MIDP + 8.0, A.mult, A.add, t_e)
+            v_e = ts(T.eoff[:], T.mis[:, 384:448], -1.0, MIDP + 7.0, A.mult, A.add, t_e)
         v_mx = st["mx"] = scan(T.srt[:, 8:], T.pka[:], T.pkb[:], NEG, A.max, A.max, v, s_w)
         tl = T["tl%d" % li]
         if sends:
-            v_t = tt(tl[:], T.srt[:].indirect(T.eoff[:]), kc[:], A.subtract, v_mx, v_e, c_kc[li])
-            need("g", v_t)
-            total = 0
-            to = [d for d in range(rank + 1, nranks) if rank in feeders(d)]
-            far = [d for d in to if not near(rank, d)]
-            for group in (to,) if FOLD else [c for c in (far[:1], [d for d in to if d not in far[:1]]) if c]:
-                trans = []
-                for d in group:
-                    srcs = [tl[:]]
-                    if feeders(d) == [rank]:
-                        srcs += [T["ld%d%d" % (li, r)][:] for r in feeders(rank)]
-                        need("g", *[landed(li, r) for r in feeders(rank)])
-                    eng = link(rank, d)
-                    total += len(eng)
-                    rid, pid = topo.addr(T.cores[d], core)
-                    trans.append(RemoteDMATransfer(dst_ids=[DstId(rid=rid, pnc=pid)], dma_engine_mask=mask_of(eng),
-                                                   remote_sem=T.sem["r%d%d" % (li, rank)], srcs=srcs,
-                                                   dsts=[T["ld%d%d" % (li, rank)][:]], alu_op=2 if len(srcs) > 1 else 0))
-                g.remote_dma_fused(trans, local_sem=T.sem["lo%d" % li])
+            total, head = 0, first_to(li, rank)
+            rest = [d for d in range(rank + 1, nranks) if d != head]
+            for group in ([head], rest):
+                for h in range(2 if group else 0):
+                    a, b = 512 * h, 512 * h + 512
+                    if group != rest:
+                        need("g", tt(tl[:, a:b], T.srt[:].indirect(T.eoff[:, a // 16:b // 16]), T.kc[:, a:b], A.subtract, v_mx, v_e, s_kc))
+                    trans = []
+                    for d in group:
+                        eng = link(rank, d)
+                        total += len(eng)
+                        rid, pid = topo.addr(T.cores[d], core)
+                        trans.append(RemoteDMATransfer(dst_ids=[DstId(rid=rid, pnc=pid)], dma_engine_mask=mask_of(eng),
+                                                       remote_sem=T.sem["r%d%d%d" % (li, rank, h)], srcs=[tl[:, a:b]],
+                                                       dsts=[T["ld%d%d" % (li, rank)][:, a:b]]))
+                    g.remote_dma_fused(trans, local_sem=T.sem["lo%d" % li])
             st["lo%d" % li] = total
         if li == 0:
-            st["zb"] = low(T.losb[:], [[0, S_TOK]], 0, 0, v_mx)
-        a = 64 if sends else 96
-        v_a = vcopy(T.los[:, 0:16 * a], T.srt[:, 8:].indirect(T.off2[:, 0:a]), v_mx)
-        s_a = sgat(T.los[:, 16 * a:], T.srt[:, 8:].indirect(T.off2[:, a:NC]), ACT.Copy, v_mx)
-        ins = feeders(rank)
+            st["zb"] = low(lo(1), [[0, S_TOK]], 0, 0, v_mx)
+        ins = list(range(1, rank))[::1 if li else -1]
+        tab = [(T["ld%d0" % li], landed(li, 0, h)) for h in range(2)] if rank else []
+
+        def direct(r):
+            return DIRECT[li] and (len(ins) == 1 or li and r == ins[-1])
 
         def to_psum():
-            for r in ins[1:]:
-                for b in range(2):
-                    kt["in", r] = mm((T.psa, T.psb)[r % 2][:, 512 * b:512 * b + 512], C(ID),
-                                     T["ld%d%d" % (li, r)][:, 512 * b:512 * b + 512], True, True, landed(li, r), s_3, v_o2)
+            for r in ins:
+                for h in range(1 if direct(r) else 2):
+                    kt["in", r, h] = mm((T.psa, T.psb)[r % 2][:, 512 * h:512 * h + 512], C(ID),
+                                        T["ld%d%d" % (li, r)][:, 512 * h:512 * h + 512], True, True, landed(li, r, h), s_3, v_o2)
+
+        def merge(r, a, b):
+            nxt, c = (T.ta, T.tb)[r % 2], slice(512 * a, 512 * b)
+            if a and direct(r):
+                t = tt(nxt[:, c], T["ld%d%d" % (li, r)][:, c], tab[a][0][:, c], A.max, landed(li, r, a), tab[a][1])
+            else:
+                t = tt(nxt[:, c], (T.psa, T.psb)[r % 2][:, c], tab[a][0][:, c], A.max, kt["in", r, b - 1], tab[a][1], tab[b - 1][1])
+            tab[a:b] = [(nxt, t)] * (b - a)
 
         if li:
             to_psum()
-        y_a = tt((T.yl if rank else out)[:, 0:CUT], T.los[:].indirect(T.off1[:, 0:CUT // 16]), T.krow[:], A.subtract, v_a, s_a)
+        ahead = ins[:-1] if li else []
+        a = 64 if sends or ahead else 96
+        v_a = vcopy(lo(0, 0, 16 * a), T.srt[:, 8:].indirect(T.off2[:, 0:a]), v_mx)
+        s_a = sgat(lo(0, 16 * a), T.srt[:, 8:].indirect(T.off2[:, a:NC]), ACT.Copy, v_mx)
+        for r in ahead:
+            merge(r, 0, 2)
+        y_a = tt((T.yl if rank else out)[:, 0:CUT], lo(0).indirect(T.off1[:, 0:CUT // 16]), T.krow[:], A.subtract, v_a, s_a)
         parts = []
         for z, c, n in banks:
-            t = sgat(T.pg[:, c - CUT:c - CUT + n], T.los[:].indirect(T.off1[:, c // 16:(c + n) // 16]), ACT.Copy, v_a, s_a)
+            t = sgat(T.pg[:, c - CUT:c - CUT + n], lo(0).indirect(T.off1[:, c // 16:(c + n) // 16]), ACT.Copy, v_a, s_a)
             parts.append((z, c, n, mm(z, T.i32[:, 0:128], T.pg[:, c - CUT:c - CUT + n], False, True, t)))
         if li == 0:
-            st["za"] = low(T.los[:], [[0, S_TOK]], 0, 0, y_a, t)
+            st["za"] = low(lo(0), [[0, S_TOK]], 0, 0, y_a, t)
             st["wm"] = ts(T.zw[:, 15:143:16], T.hm[:], T.wc[:], 1.0 / 32, A.mult, A.mult, t_w)
-            t = fill(T.ones[:], 1.0)
             for l in range(LV if rank else 0):
-                st["mkb"] = ts(T.mkb[:, NC * l:NC * l + NC], T.ones[:], T.lmk[:, l:l + 1], None, A.mult, None, t)
+                st["mkb"] = ts(T.mkb[:, NC * l:NC * l + NC], T.ones[:], T.lmk[:, l:l + 1], None, A.mult, None)
         if rank == 0:
             for z, c, n, t in parts:
                 piece_done(c, c + n, act(out[:, c:c + n], z, ACT.Copy, 0.0, 1.0, t))
             piece_done(0, CUT, y_a)
         else:
-            tin, v_in = T["ld%d%d" % (li, ins[0])], landed(li, ins[0])
             if li == 0:
                 to_psum()
-            for r in ins[1:]:
-                nxt = (T.ta, T.tb)[r % 2]
-                tin, v_in = nxt, tt(nxt[:], (T.psa, T.psb)[r % 2][:, 0:1024], tin[:], A.max, kt["in", r], v_in)
-            s_t = [sgat(T.ext[:, c:e], tin[:].indirect(T.koff[:, c // 16:e // 16]), ACT.Copy, v_in, kt["ko"])
+            for h in range(2):
+                for r in ins[len(ahead):]:
+                    merge(r, h, h + 1)
+            tin, v_in = tab[0][0], [t for _, t in tab]
+            s_t = [sgat(T.ext[:, c:e], tin[:].indirect(T.koff[:, c // 16:e // 16]), ACT.Copy, kt["ko"], *v_in)
                    for c, e in ((CUT, STORE), (STORE, S_TOK))]
             for c, e in ((0, CUT // 2), (CUT // 2, CUT)) if li else ((0, CUT),):
-                piece_done(c, e, tt(out[:, c:e], tin[:].indirect(T.koff[:, c // 16:e // 16]), T.yl[:, c:e], A.max, v_in, y_a, kt["ko"]))
+                piece_done(c, e, tt(out[:, c:e], tin[:].indirect(T.koff[:, c // 16:e // 16]), T.yl[:, c:e], A.max, y_a, kt["ko"], *v_in))
             for z, c, n, t in parts:
                 piece_done(c, c + n, tt(out[:, c:c + n], z, T.ext[:, c:c + n], A.max, t, s_t[c >= STORE]))
 

from concourse.bass import DstId, RemoteDMATransfer
from concourse.mybir import dt, AluOpType, AxisListType, ActivationFunctionType

S_TOK, NC, ND, BL = 3072, 192, 32, 12
NT = ND * BL
UNIT = 512
HI = 64 * UNIT
NEG = -1000000.0
MAGIC = 393216.0
SHIFT = 960
LIFT = 32
MIDP = 1536.0
SP_V = 96
PC = 1024
PD = 2048
SC_V = 98
CUT = 16 * SP_V
STORE = CUT + 1024
BLOCKS = {"first": (9, 5, 12), "lo": (9, 5, 12), "hi": (9, 5, 12), "ends": (7, 5, 11)}
LV = 9
ZA = 1024
ZB = 384
STEP, DIRECT = (2, 1), (1, 0)
W = 2
EARLY = 16
KF, KO = ("digit3", "digit6"), ("digit8", "digit10")
GROUPS = {"first": (10, 8, 8, 6), "lo": (8, 8, 8, 8), "hi": (10, 8, 8, 6)}
HOT_S = {"first": 0, "lo": 4, "hi": 0}
PAIR_S = {"first": 1, "lo": 1, "hi": 2}
DF, ID, I384, RD, LM, GE, BM, M3, NM = 0, 8, 9, 10, 18, 19, 20, 21, 37
PACK = (("group3", "starts", "table"), ("group3", "starts", "table"))
COPY = ({"tail": (0, 3)}, {"starts": (0, 1), "tail": (1, 3)})

SB = {"bfloat16": {"xs": S_TOK, "y1": S_TOK, "yl": CUT, "yo": S_TOK, "ext": S_TOK, "ones": NC,
                   "zero": NT, "cmod": NC, "eq": 1536, "run": NT + 16, "cnt": NT, "lsel": 16, "mkb": NC * LV,
                   "mk": 32, "mkl": 32, "cc": 64, "dsel": 32, "mrep": 1024, "e3": 1024, "tl0": 1024, "tl1": 1024,
                   "ld00": 1024, "ld01": 1024, "ld02": 1024, "ld10": 1024, "ld11": 1024, "ld12": 1024, "ta": 1024, "tb": 1024},
      "float32": {"wc": 1, "wc32": 1, "lane": 2, "one8": 8, "hm0": 8, "hm": 8, "lmk": 16, "hi192": 32, "kh": 1024, "kc": 1024,
                  "jt": 32, "ju": 32, "tab": NT, "packed": S_TOK - CUT, "pka": S_TOK, "pkb": S_TOK, "krow": CUT,
                  "x32": CUT, "pg": S_TOK - CUT, "i32": 256, "srt": S_TOK + 8},
      "int32": {"sl_i": NC, "pi": 1, "li": 1, "ri": NC, "hii": NC, "ji": 32, "cb": 32, "lb": 32},
      "float16": {"kf": NC, "pk": NC - SP_V, "gb": S_TOK, "e1": 1024},
      "uint16": {"koff": NC, "poff": NC, "off1": NC, "off2": NC, "eoff": 64, "lst": 64, "ls2": 2}}
SCRATCH = {
    "zm": ("sbuf", [128, 144], "bfloat16"), "zw": ("sbuf", [128, 144], "bfloat16"), "sl_h": ("sbuf", [128, BL, 16], "float16"),
    "sl_x": ("sbuf", [128, BL, 128], "float16"), "oh": ("sbuf", [128, ND, NC], "bfloat16"),
    "sm": ("sbuf", [128, NM, 16], "bfloat16"), "cm": ("sbuf", [128, NM, 128], "bfloat16"),
    "mrow": ("sbuf", [128, 8, 16], "bfloat16"), "row1": ("sbuf", [128, 8, 16], "bfloat16"),
    "urow": ("sbuf", [128, 8, 16], "bfloat16"), "vrow": ("sbuf", [128, 8, 16], "int32"),
    "tma": ("sbuf", [128, 8, 16], "bfloat16"), "tmb": ("sbuf", [128, 8, 16], "bfloat16"),
    "tmc": ("sbuf", [128, 8, 16], "bfloat16"),
    "dig1": ("sbuf", [128, W, NC], "bfloat16"), "dig2": ("sbuf", [128, W, NC], "bfloat16"),
    "lo": ("sbuf", [128, 2, S_TOK], "float32"), "exd": ("sbuf", [16, PD], "bfloat16"), "zs": ("sbuf", [16, 144], "bfloat16"),
    "zt": ("sbuf", [16, 8], "bfloat16"), "lft": ("sbuf", [1, 256], "bfloat16"),
    "ys": ("sbuf", [1, NT], "bfloat16"), "hrow": ("sbuf", [1, 1024], "bfloat16"), "n32": ("sbuf", [1, 128], "bfloat16"),
    "psa": ("psum", [128, 1536], "float32"), "psb": ("psum", [128, 1536], "float32"),
    "acc": ("psum", [128, 512], "float32"), "mis": ("psum", [128, 512], "float32"),
}
for _t in SB:
    for _n in SB[_t]:
        SCRATCH[_n] = ("sbuf", [128, SB[_t][_n]], _t)
LOCAL = ["dx0", "dx1", "ds", "dw", "dz", "da00", "da01", "da10", "da11", "de0", "de1"]
SEMAPHORES = (["cv", "cs", "cp", "cg", "lo0", "lo1", "dy0", "dy1", "dy2", "dy3", "dy4"] + LOCAL
              + ["r%d%d%d" % (a, b, h) for a in range(2) for b in range(3) for h in range(2)])


def mask_of(engines):
    return sum(1 << e for e in engines)


def rank_program(g, core, T, topo):
    rank = T.rank_of(core)
    if rank is None:
        return
    A, ACT = AluOpType, ActivationFunctionType
    V, S, P, Y = g.vector, g.scalar, g.tensor, g.sync
    queue = {"v": V, "s": S, "p": P, "g": g, "y": Y}
    count = {"v": 0, "s": 0, "p": 0, "g": 0}
    seen = {}
    nranks = len(T.cores)
    sends = rank < nranks - 1

    def need(q, *toks):
        best = {}
        for t in toks:
            if t is not None:
                best[t[0]] = max(best.get(t[0], 0), t[1])
        for s in sorted(best):
            if seen.get((q, s), 0) < best[s]:
                queue[q].wait_ge(T.sem[s], best[s])
                seen[(q, s)] = best[s]

    def done(q, ins):
        count[q] += 1
        ins.then_inc(T.sem["c" + q], 1)
        return ("c" + q, count[q])

    def dma(q, sem, out, in_, *deps):
        need(q, *deps)
        queue[q].dma_start(out, in_).then_inc(T.sem[sem], 16)
        return (sem, 16)

    def ts(out, in0, s1, s2, op0, op1, *deps):
        need("v", *deps)
        if op1 is None:
            return done("v", V.tensor_scalar(out, in0, s1, None, op0))
        return done("v", V.tensor_scalar(out, in0, s1, s2, op0, op1))

    def tt(out, a, b, op, *deps):
        need("v", *deps)
        return done("v", V.tensor_tensor(out, a, b, op))

    def vcopy(out, in_, *deps):
        need("v", *deps)
        return done("v", V.tensor_copy(out, in_))

    def scan(out, a, b, init, op0, op1, *deps):
        need("v", *deps)
        return done("v", V.tensor_tensor_scan(out, a, b, init, op0, op1))

    def fill(ap, c):
        return done("v", V.memset(ap, c))

    def act(out, in_, func, bias, scale, *deps):
        need("s", *deps)
        return done("s", S.activation(out, in_, func, bias=bias, scale=scale))

    def sgat(out, in_, func, *deps):
        need("s", *deps)
        return done("s", S.activation(out, in_, func))

    def mm(out, lhsT, rhs, start, stop, *deps):
        need("p", *deps)
        return done("p", P.matmul(out, lhsT, rhs, start, stop))

    def sel(out, in_, pattern, op, other, base, cm, *deps):
        need("g", *deps)
        return done("g", g.affine_select(out, in_, pattern, op, other, base, cm))

    def low(out, pattern, base, cm=0, *deps):
        need("g", *deps)
        return done("g", g.iota(out, pattern, base, cm, allow_small_or_imprecise_dtypes=True))

    def C(j):
        return T.cm[:, j, :]

    def lo(w, a=0, b=S_TOK):
        return T.lo[:, w, a:b]

    def to_lane(z, q):
        return z[:, 15 - q:143 - q]

    t_s = dma("y", "ds", T.sl_i[:], T.slot[:])
    t_x = dma("y", "dx1", T.xs[:, CUT:], T.x[:, CUT:])
    t_w = dma("y", "dw", T.wc[:], T.w[:])

    fill(T.zs[:], 0.0)
    fill(T.zt[:], 1.0 / (32.0 * HI))
    f_8 = fill(T.one8[:], 1.0)
    fill(T.zm[:], 0.0)
    fill(T.zw[:], 0.0)
    fill(T.sm[:, BM, :], 1.0)
    f_zero = fill(T.zero[:], 0.0)
    g_pi = low(T.pi[:], [[0, 1]], 0, 1)
    g_m = low(T.mrow[:], [[0, 8], [1, 16]], 0)
    t = sel(T.hm0[:], T.one8[:], [[-16, 8]], A.is_ge, 0.0, 0, 1, f_8)
    g_v = low(T.vrow[:], [[1, 8], [1, 16]], 1)
    g_u = low(T.urow[:], [[-1, 8], [1, 16]], -1)
    c_hm = sel(T.hm[:], T.hm0[:], [[16, 8]], A.is_ge, 0.0, 15, -1, t)
    g_r = sel(T.row1[:], T.mrow[:], [[-1, 8], [-1, 16]], A.is_ge, -1.0, 14, 0, g_m)
    g_q = low(T.sm[:, M3:NM, :], [[1, 16], [0, 16]], 0)
    st = {"wm": None, "mkb": None, "mx": None}
    c_kh = low(T.kh[:], [[HI // 2, 32], [UNIT // 2, 32]], SHIFT // 2)
    c_cm = low(T.cmod[:], [[0, 16], [1, BL]], 0)
    st["x32"] = dma("g", "dx0", T.x32[:], T.x[:, 0:CUT])
    t = low(lo(0, 0, ZA), [[0, ZA]], 0)
    t_z = dma("y", "dz", lo(1, 0, ZA), lo(0, 0, ZA), t)
    st["za"] = low(lo(0, ZA), [[0, S_TOK - ZA]], 0)
    st["zb"] = low(lo(1, ZA), [[0, S_TOK - ZA]], 0)
    t = sel(T.zt[:], T.zt[:], [[-2, 8]], A.is_ge, 0.0, 0, 1)
    c_zs = sel(T.zs[:, 15:143:16], T.zt[:], [[2, 8]], A.is_ge, 0.0, 1, -1, t)
    low(T.hi192[:], [[NC, 32]], 0)
    c_hi = low(T.hrow[:], [[1, 32], [0, 32]], 0)

    def spread(j0, j1, *deps):
        t = None
        for h in range(8):
            t = act(T.cm[:, j0:j1, 16 * h:16 * h + 16], T.sm[:, j0:j1, :], ACT.Copy, 0.0, T.hm[:, h:h + 1], c_hm, *deps)
        return t

    t = ts(T.li[:], T.pi[:], 15, None, A.bitwise_and, None, g_pi)
    v_l = vcopy(T.lane[:, 0:1], T.li[:], t)
    v_l2 = ts(T.lane[:, 1:2], T.li[:], -16.0, None, A.add, None, t)
    lane = T.lane[:, 0:1]
    v_v = ts(T.vrow[:], T.vrow[:], 15, None, A.bitwise_and, None, g_v)
    v_a = ts(T.tma[:], T.mrow[:], lane, None, A.is_equal, None, v_l, g_m)
    s_i = act(T.sm[:, I384, :], T.tma[:, 0, :], ACT.Silu, 0.0, float(NT), v_a)
    c_ls = ts(T.lsel[:], T.mrow[:, 0, :], lane, 1.0 / 32, A.is_equal, A.mult)
    ts(T.sm[:, ID, :], T.mrow[:, 0, :], lane, None, A.is_equal, None)
    ts(T.sm[:, LM, :], T.mrow[:, 0, :], lane, None, A.is_gt, None)
    ts(T.sm[:, GE, :], T.mrow[:, 0, :], lane, None, A.is_le, None)
    c_lk = ts(T.lmk[:], T.mrow[:, 0, :], lane, None, A.is_equal, None)
    v_b = ts(T.tmb[:], T.vrow[:], lane, None, A.is_equal, None, v_v)
    v0 = vcopy(T.sl_h[:], T.sl_i[:], t_s)
    t = tt(T.sm[:, DF:DF + 8, :], T.tma[:], T.tmb[:], A.subtract, v_b)
    c_id = spread(0, RD, t, s_i)
    for h in range(8):
        t = ts(T.sl_x[:, :, 16 * h:16 * h + 16], T.sl_h[:], T.hm[:, h:h + 1], None, A.mult, None, v0, c_hm)
    t_k = None
    for c in range(BL):
        t_k = mm(T.mis[:, c:NC:BL], T.sl_x[:, c, :], T.lsel[:], True, True, t, c_ls)
    u = ts(T.tmc[:], T.urow[:], T.lane[:, 1:2], -1.0, A.is_equal, A.mult, g_u, v_l2)
    w = ts(T.sm[:, RD:RD + 8, :], T.row1[:], lane, -1.0, A.is_equal, A.mult, g_r)
    ts(T.sm[:, M3:NM, :], T.sm[:, M3:NM, :], lane, 32.0 * UNIT, A.is_equal, A.mult, g_q)
    c_m2 = vcopy(T.zm[:, 15:143:16], T.hm[:], f_zero)
    fill(T.run[:, 0:16], 0.0)
    t = tt(T.sm[:, RD:RD + 7, :], T.sm[:, RD:RD + 7, :], T.tmc[:, 0:7, :], A.add, u, w)
    st["rd"] = spread(RD, NM, t)

    def fills(i):
        if i == 0:
            fill(T.ones[:], 1.0)
            st["ys"] = fill(T.ys[:], -4096.0)
            return
        need("v", st["ys"])
        fill(T.ys[:, 0:NT:BL], -MIDP)
        fill(T.n32[:], -1.0 / 32)
        st["zero"] = fill(T.srt[:, 0:8], NEG)

    def first_to(li, r):
        far = [d for d in range(r + 1, nranks) if not near(r, d)]
        return far[-li] if far else r + 1

    def near(a, b):
        return T.cores[a] in topo.cores_of(T.cores[b])

    def link(src, dst):
        eng = topo.engines(T.cores[src], T.cores[dst])
        if not near(src, dst):
            return eng
        far = [d for d in range(src + 1, nranks) if not near(src, d)]
        if far:
            eng = [e for e in eng if e not in topo.engines(T.cores[src], T.cores[far[0]])]
        return eng[::STEP[bool(far)]]

    def landed(li, r, h):
        return ("r%d%d%d" % (li, r, h), len(link(r, rank)))

    def sort_pass(kind, dig, off, dep, late, free, hook):
        k = {}

        def pairs(a, b, tok):
            for s in range(8):
                c = NC * s + a
                while c < NC * s + b:
                    e = min(NC * s + b, 512 * (c // 512 + 1))
                    k["df", c // 512] = mm(T.psa[:, c:e], C(DF + s), dig[:, 0, c - NC * s:e - NC * s], True, True, tok, c_id, *free)
                    c = e
            if a == 0:
                mm(T.mis[:, NC:2 * NC], C(I384), dig[:, 0, :], True, False)
                k["po"] = mm(T.mis[:, NC:2 * NC], C(ID), T.cmod[:], False, True, c_cm)

        def equal(b):
            if b < nv:
                k["eq", b] = ts(T.eq[:, 512 * b:512 * b + 512], T.psa[:, 512 * b:512 * b + 512], 0.0, None, A.is_equal, None, k["df", b])

        def equal_s():
            z = T.eq[:, 512 * nv:]
            t = act(z, T.psa[:, 512 * nv:], ACT.Square, 0.0, 32.0, k["df", 2])
            t = act(z, z, ACT.Relu, 1.0, -1.0, t)
            for b in range(nv, 3):
                k["eq", b] = t

        nv, s_oh = 3 - PAIR_S[kind], None
        if late is None:
            pairs(0, NC, dep)
            first, t_w = 4, ts(dig[:, 1, :], dig[:, 0, :], -1.0 / 32, None, A.add, None, dep)
            for e in range(ND - HOT_S[kind], ND, W):
                s_oh = act(T.oh[:, e:e + W, :], dig[:], ACT.Square, -float(e), 32.0, t_w)
            if HOT_S[kind]:
                z = T.oh[:, ND - HOT_S[kind]:, :]
                s_oh = act(z, z, ACT.Relu, 1.0, -1.0, s_oh)
            for d in range(first):
                ts(T.oh[:, d, :], dig[:, 0, :], d / 32.0, None, A.is_equal, None)
                hook("digit%d" % d, k)
        else:
            first, (n, wrapped, make) = EARLY, late
            t_w = wrapped()
            pairs(n, NC, dep)
            for d in range(0, first, W):
                if d == first - 2 * W:
                    t_w = make(t_w)
                ts(T.oh[:, d:d + W, n:], dig[:, :, n:], d / 32.0, None, A.is_equal, None, dep)
            pairs(0, n, t_w)
            equal_s()
        d = 0
        for i, n in enumerate(GROUPS[kind]):
            for e in range(d, min(d + n, ND - HOT_S[kind]), W):
                if e >= first:
                    tv = ts(T.oh[:, e:e + W, :], dig[:], e / 32.0, None, A.is_equal, None, t_w)
                    hook("digit%d" % e, k)
                elif late:
                    tv = ts(T.oh[:, e:e + W, 0:late[0]], dig[:, :, 0:late[0]], e / 32.0, None, A.is_equal, None, t_w)
            for l in range(16):
                t_tot = mm(T.acc[:, BL * d:BL * (d + n)], to_lane(T.zm, l), T.oh[:, d:d + n, BL * l:BL * l + BL], l == 0, l == 15,
                           tv, c_m2, s_oh if d + n > ND - HOT_S[kind] else None, *free)
            d += n
            if i == 3:
                mm(T.psb[:, 1024:1024 + NT], T.ones[0:1, 0:128], T.ys[:], True, False, st["zero"])
            hook("group%d" % i, k)
            if kind != "hi" and i == 1:
                equal_s()
        v_po = vcopy(T.poff[:], T.mis[:, NC:2 * NC], k["po"])
        equal(0)
        v_run = scan(T.run[:, 1:NT + 1], T.acc[:, 0:NT], T.zero[:, 0:NT], 0.0, A.add, A.add, t_tot, st["zero"])
        v_cnt = vcopy(T.cnt[:], T.acc[:, 0:NT])
        mm(T.psb[:, 1024:1024 + NT:BL], C(GE), T.run[:, 0:NT:BL], False, False, v_run, st["rd"])
        t = mm(T.psb[:, 1024:1024 + NT:BL], C(LM), T.run[:, BL:NT + 1:BL], False, True)
        if kind != "hi" and sends:
            k["ends"] = mm(T.acc[:, NT + 32:NT + 64], C(BM), T.run[:, BL:NT + 1:BL], True, True, v_cnt)
        hook("starts", k)
        equal(1)
        v_tab = k["tab"] = scan(T.tab[:], T.psb[:, 1024:1024 + NT], T.cnt[:], -4096.0, A.max, A.add, t, v_cnt)
        equal(2)

        def gather(l0, l1):
            t = None
            if l0 >= lv:
                for l in range(l0, l1):
                    t = act(T.gb[:, NC * l:NC * l + NC], T.tab[:].indirect(T.poff[:, BL * l:BL * l + BL]), ACT.Copy, 0.0,
                            T.lmk[:, l:l + 1], v_tab, v_po, c_lk)
            elif st["mkb"] is None:
                for l in range(l0, l1):
                    t = ts(T.gb[:, NC * l:NC * l + NC], T.tab[:].indirect(T.poff[:, BL * l:BL * l + BL]), T.lmk[:, l:l + 1], None,
                           A.mult, None, v_tab, v_po)
            else:
                t = tt(T.gb[:, NC * l0:NC * l1], T.tab[:].indirect(T.poff[:, BL * l0:BL * l1]), T.mkb[:, NC * l0:NC * l1], A.mult,
                       v_tab, v_po, st["mkb"])
            return t

        def wrap(l0, l1, *deps):
            a, b, t = BL * l0, BL * l1, None
            for q in range(16):
                t = mm(T.mis[:, a:b], to_lane(T.zm, q), T.gb[:, 16 * a + q:16 * b:16], False, q == 15 and len(deps) == 2, *deps)
            return t

        lv, l1, l2 = BLOCKS["ends" if kind == "hi" and sends else kind]
        hook("table", k)
        for s in range(8):
            mm(T.mis[:, 0:NC], C(RD + s), T.eq[:, NC * s:NC * s + NC], s == 0, False, v_po, k["eq", NC * s // 512],
               k["eq", (NC * s + NC - 1) // 512])
        ga, gs = gather(0, l1), gather(l2, 16)
        hook("mid", k)
        gb, gt = gather(l1, lv), gather(lv, l2)
        wrap(0, l1, ga)
        wrap(l2, 16, gs)
        t = wrap(l1, l2, gb, gt)
        hook("tail", k)
        k["off"] = ts(off[:], T.mis[:, 0:NC], MIDP - 1.0, None, A.add, None, t)
        hook("off", k)
        return k

    def layer(li, src, src_toks, key_tok, out, piece_done):
        shift = float(SHIFT + li * LIFT * HI)
        v_ri = ts(T.ri[:], T.mis[:, 0:NC], -31.0 / 64, None, A.add, None, key_tok)
        if li == 0:
            fills(0)
        v_d1 = tt(T.dig1[:, 0, :], T.mis[:, 0:NC], T.ri[:], A.subtract, v_ri)
        kt = {}
        hi, v_hi = T.ri, v_ri
        if li:
            hi, v_hi = T.hii, ts(T.hii[:], T.ri[:], 31, None, A.bitwise_and, None, v_ri)

        def hook1(name, k):
            if name == KF[li]:
                kt["kf"] = tt(T.kf[:], hi[:], T.dig1[:, 0, :], A.add, v_hi)
            if name == KO[li]:
                kt["ko"] = ts(T.koff[:], T.kf[:], 32.0, None, A.mult, None, kt["kf"])
                kt["kr"] = act(T.krow[:], T.kh[:].indirect(T.koff[:, 0:SP_V]), ACT.Copy, shift - SHIFT, 2.0, kt["ko"], c_kh)
                kt["pk"] = tt(T.pk[:], hi[:, SP_V:], T.kf[:, SP_V:], A.add)
            for i in range(3):
                if name == PACK[li][i]:
                    mm(T.psb[:, 512 * i:512 * i + 512], C(ID), src[:, CUT + 512 * i:CUT + 512 * i + 512], True, False, st["rd"],
                       k.get("tab"), *src_toks)
                    for q in range(16):
                        kt["pb", i] = mm(T.psb[:, 512 * i + q:512 * i + 512:16], C(M3 + q), T.pk[:, 32 * i:32 * i + 32], False,
                                         q == 15, kt["pk"])
            if name in COPY[li]:
                a, b = COPY[li][name]
                kt["pa"] = act(T.packed[:, 512 * a:512 * b], T.psb[:, 512 * a:512 * b], ACT.Copy, shift, 1.0, kt["pb", b - 1])
            if name == "digit3" and li == 0:
                fills(1)
            if name == "tail" and li == 0:
                for i in range(2):
                    fill(T.lft[:, 128 * i:128 * i + 128], i * LIFT + 0.25)
            if not sends:
                return
            if name == "table":
                kt["ji"] = ts(T.ji[:], T.acc[:, NT + 32:NT + 64], -1.0, 0.0, A.add, A.max, k["ends"])
            if name == "mid":
                kt["cb"] = ts(T.cb[:], T.ji[:], 4, None, A.logical_shift_right, None, kt["ji"])
            if name == "tail":
                ts(T.jt[:], T.cb[:], 16.0, lane, A.mult, A.add, kt["cb"])
                vcopy(T.cc[:, 0:32], T.cb[:])
                t = ts(T.lb[:], T.cb[:], 1.0 / BL, -11.0 / 24, A.mult, A.add)
                kt["mk"] = tt(T.mk[:], T.jt[:], T.acc[:, NT + 32:NT + 64], A.is_lt, t)
                kt["mkl"] = ts(T.mkl[:], T.lb[:], lane, -1.0, A.is_equal, A.mult)
                kt["ju"] = ts(T.ju[:], T.lb[:], -float(BL), None, A.mult, None)
            if name == "off":
                kt["cc"] = tt(T.cc[:, 32:64], T.ju[:], T.cb[:], A.add, kt["ju"])

        k1 = sort_pass("lo" if li else "first", T.dig1, T.off1, v_d1, None, [st["mx"]], hook1)
        v_o1 = k1["off"]
        if li == 0:
            vcopy(T.i32[:, 0:128], C(ID), c_id)
            st["i32"] = ts(T.i32[:, 128:256], C(ID), -1.0, None, A.mult, None)
        v_s1 = tt(lo(0).indirect(T.off1[:, 0:SP_V]), T.krow[:], T.x32[:], A.add, v_o1, st["za"], kt["kr"], st["x32"], t_z)
        s_s1 = sgat(lo(1).indirect(T.off1[:, SP_V:NC]), T.packed[:], ACT.Silu, v_o1, st["zb"], kt["pa"], t_z)
        if sends:
            for q in range(16):
                t = mm(T.psb[:, 1024:1028], to_lane(T.zm, q), T.cc[:, q:64:16], q == 0, q == 15, kt["cc"], kt["pa"])
            for i in range(32):
                t_rep = mm(T.psb[:, 32 * i:32 * i + 32], C(ID), T.mkl[:], True, True, kt["mkl"])
            for b in range(2):
                ts(T.lst[:, b:64:2], T.hi192[:], T.psb[:, 1026 + b:1027 + b], 1.0 / 16, A.add, A.mult, t, c_hi)
            kt["l"] = ts(T.ls2[:], T.psb[:, 1024:1026], 1.0 / 16, None, A.mult, None)
        t_dm = dma("g", "de%d" % li, T.exd[:], T.lo[0:128:16, :, 0:PD], v_s1, s_s1)
        t_hi, t_ea, sc_hi, lift = {}, [], 1.0 / (512.0 * HI), -(li * LIFT + 0.25) / 1024.0
        need("v", v_s1)
        need("s", s_s1)
        for c in range(S_TOK - PC, PD - 1, -PC):
            e_a = ts(T.ext[:, c:c + PC], lo(0, c, c + PC), sc_hi, lift, A.mult, A.add)
            t_ea.append(e_a)
            e_b = act(T.yo[:, c:c + PC], lo(1, c, c + PC), ACT.Copy, lift, sc_hi)
            for last, x, t in ((False, T.ext, e_a), (True, T.yo, e_b)):
                for q in range(16):
                    t_hi[c] = mm(T.mis[:, c // 16:(c + PC) // 16], to_lane(T.zm, q), x[:, c + q:c + PC:16],
                                 q == 0 and not last, q == 15 and last, t, v_o1)

        def late():
            mm(T.acc[:, 0:PD // 16], T.n32[:], T.lft[:, 128 * li:128 * li + PD // 16], True, False, v_o1)
            for q in range(16):
                t = mm(T.acc[:, 0:PD // 16], to_lane(T.zs, q), T.exd[:, q:PD:16], False, q == 15, t_dm, c_zs)
            return t

        t_da = []
        for a, b, t in ((S_TOK - PC, S_TOK, t_ea[0]), (16 * SC_V, S_TOK - PC, t_dm if PD > 16 * SC_V else t_ea[1])):
            if li == 0:
                z = ZB * len(t_da)
                low(T.pka[:, z:z + ZB], [[0, ZB]], 0)
            need("g", t)
            g.dma_start(lo(0, a, b), lo(1, a, b), accum_op=A.add).then_inc(T.sem["da%d%d" % (li, len(t_da))], 16)
            t_da.append(("da%d%d" % (li, len(t_da)), 16))
        if li == 0:
            low(T.pka[:, 2 * ZB:], [[0, S_TOK - 2 * ZB]], 0)
            st["zw"] = low(T.pkb[:], [[0, S_TOK]], 0)
        if sends:
            s_rep = act(T.mrep[:], T.psb[:, 0:1024], ACT.Copy, 0.0, 1.0, t_rep)
            s_kc = act(T.kc[:], T.kh[:], ACT.Copy, shift - SHIFT, 2.0, st["mx"])

        def rounded(ps, a, b, tok):
            return [ts(T.dig2[:, r, a:b], ps[:, a:b], MAGIC, MAGIC + r / 32.0, A.add, A.subtract, tok) for r in range(W)]

        def hook2(name, k):
            if not sends:
                return
            if name == "group0":
                kt["ds"] = tt(T.dsel[:], T.dig2[:, 0, :].indirect(T.ls2[:]), T.mk[:], A.add, kt["l"])
            if name == "group3":
                for b in (1, 0):
                    mm(T.psb[:, 512 * b:512 * b + 512], T.n32[:], T.hrow[:, 512 * b:512 * b + 512], True, False, s_rep, c_hi)
                    for i in range(16):
                        c = 512 * b + 32 * i
                        kt["z", b] = mm(T.psb[:, c:c + 32], C(ID), T.dsel[:], False, i == 15, kt["ds"])
                t = act(T.e3[:, 512:], T.psb[:, 512:1024], ACT.Square, 0.0, 32.0, kt["z", 1])
                kt["e2"] = act(T.e3[:, 512:], T.e3[:, 512:], ACT.Relu, 1.0, -1.0, t)
            if name == "table":
                kt["e3"] = ts(T.e3[:, 0:512], T.psb[:, 0:512], 0.0, None, A.is_equal, None, kt["z", 0])
            if name == "tail":
                kt["e1"] = tt(T.e1[:], T.tab[:].indirect(T.lst[:]), T.mrep[:], A.mult, k["tab"], s_rep)

        n = PD // 16
        k2 = sort_pass("hi", T.dig2, T.off2, rounded(T.mis, n, NC, t_hi[PD])[1], (n, late, lambda t: rounded(T.acc, 0, n, t)[1]),
                       [], hook2)
        v_o2 = k2["off"]
        s_3 = kt.get("e2")
        if sends:
            for i, e in enumerate((T.e1, T.e3)):
                for q in range(16):
                    t_e = mm(T.mis[:, 384:448], to_lane(T.zm, q), e[:, q:1024:16], i + q == 0, i + q == 16, kt["e1"], kt["e2"], v_o2)
        need("v", v_o2, st["zw"], v_s1, s_s1)
        v = done("v", V.tensor_tensor(T.pka[:].indirect(T.off2[:, 0:SC_V]), lo(0, 0, 16 * SC_V), lo(1, 0, 16 * SC_V), A.add))
        s_w = sgat(T.pkb[:].indirect(T.off2[:, SC_V:NC]), lo(0, 16 * SC_V), ACT.Silu, v_o2, st["zw"], *t_da)
        banks = []
        for i, (ps, o) in enumerate(((T.acc, 0), (T.psa, 1024), (T.psb, 1024))):
            c = CUT + 512 * i
            n = min(512, S_TOK - c)
            banks.append((ps[:, o:o + n], c, n))
            mm(ps[:, o:o + n], C(ID), src[:, c:c + n], True, False, v_o2, *src_toks)
            mm(ps[:, o:o + n], T.i32[:, 128:256], T.packed[:, c - CUT:c - CUT + n], False, False, st["i32"])
        if sends:
            v_e = ts(T.eoff[:], T.mis[:, 384:448], -1.0, MIDP + 7.0, A.mult, A.add, t_e)
        v_mx = st["mx"] = scan(T.srt[:, 8:], T.pka[:], T.pkb[:], NEG, A.max, A.max, v, s_w)
        tl = T["tl%d" % li]
        if sends:
            total, head = 0, first_to(li, rank)
            rest = [d for d in range(rank + 1, nranks) if d != head]
            for group in ([head], rest):
                for h in range(2 if group else 0):
                    a, b = 512 * h, 512 * h + 512
                    if group != rest:
                        need("g", tt(tl[:, a:b], T.srt[:].indirect(T.eoff[:, a // 16:b // 16]), T.kc[:, a:b], A.subtract, v_mx, v_e, s_kc))
                    trans = []
                    for d in group:
                        eng = link(rank, d)
                        total += len(eng)
                        rid, pid = topo.addr(T.cores[d], core)
                        trans.append(RemoteDMATransfer(dst_ids=[DstId(rid=rid, pnc=pid)], dma_engine_mask=mask_of(eng),
                                                       remote_sem=T.sem["r%d%d%d" % (li, rank, h)], srcs=[tl[:, a:b]],
                                                       dsts=[T["ld%d%d" % (li, rank)][:, a:b]]))
                    g.remote_dma_fused(trans, local_sem=T.sem["lo%d" % li])
            st["lo%d" % li] = total
        if li == 0:
            st["zb"] = low(lo(1), [[0, S_TOK]], 0, 0, v_mx)
        ins = list(range(1, rank))[::1 if li else -1]
        tab = [(T["ld%d0" % li], landed(li, 0, h)) for h in range(2)] if rank else []

        def direct(r):
            return DIRECT[li] and (len(ins) == 1 or li and r == ins[-1])

        def to_psum():
            for r in ins:
                for h in range(1 if direct(r) else 2):
                    kt["in", r, h] = mm((T.psa, T.psb)[r % 2][:, 512 * h:512 * h + 512], C(ID),
                                        T["ld%d%d" % (li, r)][:, 512 * h:512 * h + 512], True, True, landed(li, r, h), s_3, v_o2)

        def merge(r, a, b):
            nxt, c = (T.ta, T.tb)[r % 2], slice(512 * a, 512 * b)
            if a and direct(r):
                t = tt(nxt[:, c], T["ld%d%d" % (li, r)][:, c], tab[a][0][:, c], A.max, landed(li, r, a), tab[a][1])
            else:
                t = tt(nxt[:, c], (T.psa, T.psb)[r % 2][:, c], tab[a][0][:, c], A.max, kt["in", r, b - 1], tab[a][1], tab[b - 1][1])
            tab[a:b] = [(nxt, t)] * (b - a)

        if li:
            to_psum()
        ahead = ins[:-1] if li else []
        a = 64 if sends or ahead else 96
        v_a = vcopy(lo(0, 0, 16 * a), T.srt[:, 8:].indirect(T.off2[:, 0:a]), v_mx)
        s_a = sgat(lo(0, 16 * a), T.srt[:, 8:].indirect(T.off2[:, a:NC]), ACT.Copy, v_mx)
        for r in ahead:
            merge(r, 0, 2)
        y_a = tt((T.yl if rank else out)[:, 0:CUT], lo(0).indirect(T.off1[:, 0:CUT // 16]), T.krow[:], A.subtract, v_a, s_a)
        parts = []
        for z, c, n in banks:
            t = sgat(T.pg[:, c - CUT:c - CUT + n], lo(0).indirect(T.off1[:, c // 16:(c + n) // 16]), ACT.Copy, v_a, s_a)
            parts.append((z, c, n, mm(z, T.i32[:, 0:128], T.pg[:, c - CUT:c - CUT + n], False, True, t)))
        if li == 0:
            st["za"] = low(lo(0), [[0, S_TOK]], 0, 0, y_a, t)
            st["wm"] = ts(T.zw[:, 15:143:16], T.hm[:], T.wc[:], 1.0 / 32, A.mult, A.mult, t_w)
            for l in range(LV if rank else 0):
                st["mkb"] = ts(T.mkb[:, NC * l:NC * l + NC], T.ones[:], T.lmk[:, l:l + 1], None, A.mult, None)
        if rank == 0:
            for z, c, n, t in parts:
                piece_done(c, c + n, act(out[:, c:c + n], z, ACT.Copy, 0.0, 1.0, t))
            piece_done(0, CUT, y_a)
        else:
            if li == 0:
                to_psum()
            for h in range(2):
                for r in ins[len(ahead):]:
                    merge(r, h, h + 1)
            tin, v_in = tab[0][0], [t for _, t in tab]
            s_t = [sgat(T.ext[:, c:e], tin[:].indirect(T.koff[:, c // 16:e // 16]), ACT.Copy, kt["ko"], *v_in)
                   for c, e in ((CUT, STORE), (STORE, S_TOK))]
            for c, e in ((0, CUT // 2), (CUT // 2, CUT)) if li else ((0, CUT),):
                piece_done(c, e, tt(out[:, c:e], tin[:].indirect(T.koff[:, c // 16:e // 16]), T.yl[:, c:e], A.max, y_a, kt["ko"], *v_in))
            for z, c, n, t in parts:
                piece_done(c, c + n, tt(out[:, c:c + n], z, T.ext[:, c:c + n], A.max, t, s_t[c >= STORE]))

    hk, last, stores = [], {}, []

    def hash_piece(c, e, tok):
        t = None
        for q in range(16):
            t = mm(T.mis[:, c // 16:e // 16], to_lane(T.zw, q), T.y1[:, c + q:e:16], q == 0, q == 15, tok, st["wm"])
        if c == 0:
            st["x32"] = act(T.x32[:], T.y1[:, 0:CUT], ACT.Copy, 0.0, 1.0, tok)
        hk.append((tok, t))

    def joined(piece):
        def f(c, e, tok):
            if c == CUT:
                last["tok"] = tok
            elif e == STORE:
                piece(CUT, STORE, tok)
            else:
                piece(c, e, tok)
        return f

    def store_piece(c, e, tok):
        stores.append(dma("y", "dy%d" % len(stores), T.y[:, c:e], T.yo[:, c:e], tok))

    layer(0, T.xs, [t_x], t_k, T.y1, joined(hash_piece))
    layer(1, T.y1, [h[0] for h in hk], max(h[1] for h in hk), T.yo, joined(store_piece))

    for q in ("v", "s", "p", "g"):
        need("g", ("c" + q, count[q]))
    for s in LOCAL:
        need("g", (s, 16))
    need("g", *stores)
    if sends:
        for li in range(2):
            need("g", ("lo%d" % li, st["lo%d" % li]))
